import numpy as np
import ml_dtypes


def mxq(x, axis, fmt="e4m3"):
    dtype, down = {"e4m3": (ml_dtypes.float8_e4m3fn, 7), "e5m2": (ml_dtypes.float8_e5m2, 14)}[fmt]
    v = np.moveaxis(np.asarray(x, np.float32).astype(ml_dtypes.bfloat16).astype(np.float64), axis, -1)
    blocks = v.reshape(v.shape[:-1] + (-1, 32))
    amax = np.abs(blocks).max(-1, keepdims=True)
    byte = np.maximum(np.where(amax > 0, np.frexp(amax)[1] - 1 + 127, 0) - down, 1)
    scale = np.exp2(byte - 127.0)
    codes = (blocks / scale).astype(np.float32).astype(dtype).astype(np.float64)
    return np.moveaxis((codes * scale).reshape(v.shape), -1, axis)


WIDE = False


def mx_kscale(k):
    if not WIDE:
        return np.ones(k)
    levels = np.array([10, -10, 5, -5, 0])
    if k % 512:
        return np.exp2(np.random.permutation(np.resize(levels, k // 32))).repeat(32)
    a = np.empty((k // 512, 16))
    for p in range(k // 512):
        a[p, :8] = np.random.permutation(np.resize(levels, 8))
        for g in range(8):
            far = levels[np.abs(levels - a[p, g]) >= 10]
            a[p, g + 8] = far[np.random.randint(len(far))]
    return np.exp2(a.ravel()).repeat(32)


def f64(x):
    return np.asarray(x).astype(np.float64)


def striped(idx):
    return np.tile(np.asarray(idx).reshape(-1, 16).T, (8, 1)).astype(np.uint16)


def unstriped(offs):
    return offs[:16].T.reshape(-1).astype(np.int64)


E2M1 = np.array([0.0, 0.5, 1.0, 1.5, 2.0, 3.0, 4.0, 6.0, -0.0, -0.5, -1.0, -1.5, -2.0, -3.0, -4.0, -6.0])


def pack_weight(w, fmt):
    k, n = w.shape
    w = f64(np.asarray(w, np.float32).astype(ml_dtypes.bfloat16)).reshape(k // 32, 32, n)
    amax = np.abs(w).max(1)
    if fmt == "e4m3":
        byte = np.frexp(amax)[1] - 1 + 127 - 7
    else:
        mant, ex = np.frexp(amax / 6.0)
        byte = np.where(mant > 0.5, ex, ex - 1) + 127
    byte = np.clip(np.where(amax > 0, byte, 1), 1, 254)
    scaled = (w * np.exp2(127.0 - byte)[:, None, :]).reshape(k, n).astype(np.float32)
    by_word = np.ascontiguousarray(scaled.reshape(k // 512, 128, 4, n).transpose(0, 1, 3, 2))
    if fmt == "e4m3":
        words = by_word.astype(ml_dtypes.float8_e4m3fn).view(np.uint8)
    else:
        c = by_word.astype(ml_dtypes.float4_e2m1fn).view(np.uint8) & 0xF
        words = (c[..., 0::2] | (c[..., 1::2] << 4)).reshape(k // 512, 128, 2 * n)
    return np.ascontiguousarray(words), np.ascontiguousarray(byte.astype(np.uint8).reshape(k // 512, 16, n))


def unpack_weight(words, scales, fmt):
    g, _, n = scales.shape
    words = np.ascontiguousarray(words).reshape(g, 128, n, -1)
    if fmt == "e4m3":
        vals = words.view(ml_dtypes.float8_e4m3fn).astype(np.float64)
    else:
        nib = np.empty((g, 128, n, 4), np.uint8)
        nib[..., 0::2] = words & 0xF
        nib[..., 1::2] = words >> 4
        vals = E2M1[nib]
    vals = vals * np.repeat(np.exp2(scales.astype(np.float64) - 127.0), 8, axis=1)[..., None]
    return vals.transpose(0, 1, 3, 2).reshape(g * 512, n)


D, K, T, I, V, Q = 512, 512, 2048, 512, 1024, 128


def setup_inputs():
    n = np.random.standard_normal
    idx = np.random.permutation(T)[:I]
    idx2 = np.random.permutation(V)[:I]
    fd = mx_kscale(D)
    fk = mx_kscale(K)
    keysp = pack_weight(n((D, T)) / fd[:, None], "e4m3")
    return {
        "query": (n((D, Q)) * 0.5 / np.sqrt(D) * fd[:, None]).astype(np.float32),
        "keys_words": keysp[0],
        "keys_scales": keysp[1],
        "kn": np.tile(np.random.uniform(0.0, 1.0, T), (128, 1)).astype(np.float32),
        "hid": (n((K, Q)) * 1.0 / np.sqrt(K) * fk[:, None]).astype(np.float32),
        "voc": (n((K, V)) / fk[:, None]).astype(np.float32),
        "lam": (np.random.uniform(0.2, 0.8, (Q, 1))).astype(np.float32),
        "offs": striped(idx),
        "offs2": striped(idx2),
    }


def reference(query, keys_words, keys_scales, kn, hid, voc, lam, offs, offs2):
    idx = unstriped(offs)
    idx2 = unstriped(offs2)
    keysu = unpack_weight(keys_words, keys_scales, "e4m3")
    queryq = mxq(f64(query), 0, "e4m3")
    keysidxg = keysu[:, idx]
    a = queryq.T @ keysidxg
    s = 2.0 * a - f64(kn)[:1][:, idx]
    p = np.exp(s - np.max(s, axis=1, keepdims=True))
    w = p / np.sum(p, axis=1, keepdims=True)
    wf = np.zeros((Q, V))
    wf[:, idx2] = w
    hidq = mxq(f64(hid), 0, "e4m3")
    vocq = mxq(f64(voc), 0, "e4m3")
    b = hidq.T @ vocq
    r = np.exp(b - np.max(b, axis=1, keepdims=True))
    y = (f64(lam) * wf + (1.0 - f64(lam)) * r / np.sum(r, axis=1, keepdims=True)) * 512.0
    return y

@@ -1,0 +1,228 @@
+from contextlib import ExitStack
+
+import concourse.mybir as mybir
+
+D, K, T, I, V, Q = 512, 512, 2048, 512, 1024, 128
+FLOPS = 2 * D * Q * I + 2 * K * Q * V
+
+F32 = mybir.dt.float32
+BF16 = mybir.dt.bfloat16
+I32 = mybir.dt.int32
+U32 = mybir.dt.uint32
+U16 = mybir.dt.uint16
+U8 = mybir.dt.uint8
+FP8X4 = mybir.dt.float8_e4m3fn_x4
+ALU = mybir.AluOpType
+ACT = mybir.ActivationFunctionType
+AX = mybir.AxisListType
+
+P = 128
+PACK = 4
+LANES = 16
+KN_ROW = 8
+VOC_CHUNK = 256
+GROUPS = ((0, 512), (512, 768), (768, 1024))
+KEY_HALF = 256
+CAST_COLS = 128
+SCATTER_PIECE = 128
+
+
+def tile_attend_knnlm_kernel(tc, query, keys_words, keys_scales, kn, hid, voc, lam, offs, offs2, out):
+    nc = tc.nc
+    with ExitStack() as ctx:
+        sb = ctx.enter_context(tc.tile_pool(name="sb", bufs=1))
+        ps = ctx.enter_context(tc.psum_pool(name="ps", bufs=1))
+
+        def load_rows(flat, rows):
+            raw = flat.rearrange("p (j w) -> p j w", j=PACK)
+            nc.sync.dma_start(out=raw, in_=rows.rearrange("(p j) w -> p j w", j=PACK))
+            return raw
+
+        def cast(name, raw, on_vector=False):
+            width = raw.shape[2]
+            grouped = sb.tile([P, width, PACK], BF16, name=name + "_bf", align_bytes=64)
+            step = width if on_vector else CAST_COLS
+            for c0 in range(0, width, step):
+                dst = grouped[:, c0 : c0 + step, :].rearrange("p (c i) t -> p c t i", i=4)
+                src = raw[:, :, c0 : c0 + step].rearrange("p t (c i) -> p c t i", i=4)
+                if on_vector:
+                    nc.vector.tensor_copy(out=dst, in_=src)
+                else:
+                    nc.scalar.activation(out=dst, in_=src, func=ACT.Copy)
+            return grouped
+
+        def quantize(name, grouped):
+            width = grouped.shape[1]
+            codes = sb.tile([P, width], U32, name=name + "_codes", align_bytes=64)
+            scales = sb.tile([P, width], U8, name=name + "_scales", align_bytes=64)
+            nc.vector.quantize_mx(
+                out=codes[:].bitcast(FP8X4), scales=scales[:], in_=grouped[:].rearrange("p w t -> p (w t)")
+            )
+            return codes, scales
+
+        scale_pool = sb.tile([P, T], U8, name="scale_pool", align_bytes=64)
+        kn_pool = sb.tile([P, T], F32, name="kn_pool", tag="kn_then_words", align_bytes=64)
+        word_pool = sb.tile([P, T], I32, name="word_pool")
+        wf = sb.tile([P, V], F32, name="wf")
+        ident = sb.tile([P, P], F32, name="ident")
+        key_list = sb.tile([P, I // LANES], U16, name="key_list")
+        place_list = sb.tile([P, I // LANES], U16, name="place_list")
+        zeros = sb.tile([P, P], F32, name="zeros", tag="late")
+
+        nc.vector.memset(scale_pool[:].bitcast(I32), 0)
+        nc.vector.memset(kn_pool[:], 0.0)
+        nc.vector.memset(zeros[:], 0.0)
+        nc.vector.memset(wf[:], 0.0)
+        nc.gpsimd.affine_select(
+            out=ident[:], in_=zeros[:], compare_op=ALU.not_equal, fill=1.0, base=0, pattern=[[-1, P]], channel_multiplier=1
+        )
+
+        nc.sync.dma_start(key_list[:], offs)
+        query_flat = sb.tile([P, PACK * Q], F32, name="query_flat")
+        query_raw = load_rows(query_flat[:], query)
+        nc.scalar.dma_start(out=word_pool[:], in_=keys_words[0].rearrange("p n t -> p (n t)").bitcast(I32))
+        for quad in range(4):
+            nc.sync.dma_start(
+                out=scale_pool[32 * quad : 32 * quad + 4, :].bitcast(I32),
+                in_=keys_scales[0, 4 * quad : 4 * quad + 4, :].bitcast(I32),
+            )
+        nc.sync.dma_start(out=kn_pool[KN_ROW : KN_ROW + 1, :], in_=kn[0:1, :])
+        nc.sync.dma_start(place_list[:], offs2)
+        n_chunks = V // VOC_CHUNK
+        late = sb.tile([P, PACK * (Q + V) + 8], F32, name="late", tag="late")
+        hid_raw = load_rows(late[:, 0 : PACK * Q], hid)
+        voc_raw = []
+        for c in range(n_chunks):
+            c0 = c * VOC_CHUNK
+            voc_raw.append(load_rows(late[:, PACK * (Q + c0) : PACK * (Q + c0 + VOC_CHUNK)], voc[:, c0 : c0 + VOC_CHUNK]))
+        lam_sb = late[:, PACK * (Q + V) : PACK * (Q + V) + 1]
+        nc.sync.dma_start(out=lam_sb, in_=lam)
+
+        key_scales = sb.tile([P, I], U8, name="key_scales", align_bytes=64)
+        nc.vector.tensor_copy(key_scales[:], scale_pool[:].indirect(key_list[:]))
+        kn_listed = sb.tile([P, I], F32, name="kn_listed")
+        nc.vector.tensor_copy(kn_listed[:], kn_pool[:].indirect(key_list[:]))
+        query_bf = cast("query", query_raw)
+        query_codes, query_scales = quantize("query", query_bf)
+
+        kn_turned = ps.tile([P, I // P, P], F32, name="kn_turned")
+        for j in range(I // P):
+            nc.tensor.transpose(kn_turned[:, j, :], kn_listed[:, j * P : (j + 1) * P], ident[:])
+        neg_kn = sb.tile([P, I // P], F32, name="neg_kn")
+        nc.scalar.activation(out=neg_kn[:], in_=kn_turned[:, :, KN_ROW], func=ACT.Identity, scale=-1.0)
+
+        hid_bf = cast("hid", hid_raw)
+        s_ps = ps.tile([P, I], F32, name="s_ps")
+        key_words = sb.tile([P, I], I32, name="key_words", tag="kn_then_words", align_bytes=64)
+        for h in range(I // KEY_HALF):
+            cols = KEY_HALF // LANES
+            nc.vector.tensor_copy(
+                key_words[:, h * KEY_HALF : (h + 1) * KEY_HALF].bitcast(U32),
+                word_pool[:].bitcast(U32).indirect(key_list[:, h * cols : (h + 1) * cols]),
+            )
+            a_ps = ps.tile([P, KEY_HALF // P, Q], F32, name="a_ps%d" % h)
+            s_turned = sb.tile([P, KEY_HALF // P, Q], F32, name="s_turned%d" % h)
+            for u in range(KEY_HALF // P):
+                j = h * (KEY_HALF // P) + u
+                nc.tensor.matmul_mx(
+                    out=a_ps[:, u, :],
+                    lhsT=key_words[:, j * P : (j + 1) * P].bitcast(FP8X4),
+                    lhsT_scale=key_scales[:, j * P : (j + 1) * P],
+                    rhs=query_codes[:].bitcast(FP8X4),
+                    rhs_scale=query_scales[:],
+                    start=True,
+                    stop=True,
+                )
+            for u in range(KEY_HALF // P):
+                j = h * (KEY_HALF // P) + u
+                nc.scalar.activation(
+                    out=s_turned[:, u, :], in_=a_ps[:, u, :], func=ACT.Identity, scale=2.0, bias=neg_kn[:, j : j + 1]
+                )
+            for u in range(KEY_HALF // P):
+                j = h * (KEY_HALF // P) + u
+                nc.tensor.transpose(s_ps[:, j * P : (j + 1) * P], s_turned[:, u, :], ident[:])
+
+        neg_max = sb.tile([P, 1], F32, name="neg_max")
+        nc.vector.tensor_reduce(out=neg_max[:], in_=s_ps[:], axis=AX.X, op=ALU.max, negate=True)
+        n_pieces = I // SCATTER_PIECE
+        p_sums = sb.tile([P, n_pieces], F32, name="p_sums")
+
+        def knn_piece(c):
+            p_sb = sb.tile([P, SCATTER_PIECE], F32, name="p_sb%d" % c)
+            nc.scalar.activation(
+                out=p_sb[:],
+                in_=s_ps[:, c * SCATTER_PIECE : (c + 1) * SCATTER_PIECE],
+                func=ACT.Exp,
+                bias=neg_max[:],
+                accum_out=p_sums[:, c : c + 1],
+            )
+            cols = SCATTER_PIECE // LANES
+            nc.vector.tensor_copy(wf[:].indirect(place_list[:, c * cols : (c + 1) * cols]), p_sb[:])
+
+        lm_share = sb.tile([P, 1], F32, name="lm_share")
+        nc.gpsimd.tensor_scalar(lm_share[:], lam_sb, -512.0, 512.0, ALU.mult, ALU.add)
+
+        hid_codes, hid_scales = quantize("hid", hid_bf)
+        b_ps = [ps.tile([P, hi - lo], F32, name="b_ps%d" % g) for g, (lo, hi) in enumerate(GROUPS)]
+        neg_b = sb.tile([P, len(GROUPS)], F32, name="neg_b")
+        r_sum = sb.tile([P, len(GROUPS)], F32, name="r_sum")
+        r_sb = [sb.tile([P, hi - lo], F32, name="r_sb%d" % g) for g, (lo, hi) in enumerate(GROUPS)]
+
+        def lm_chunk(c):
+            codes, scales = quantize("voc%d" % c, cast("voc%d" % c, voc_raw[c], on_vector=(c == 0)))
+            c0 = c * VOC_CHUNK
+            g = [n for n, (lo, hi) in enumerate(GROUPS) if lo <= c0 < hi][0]
+            lo, hi = GROUPS[g]
+            nc.tensor.matmul_mx(
+                out=b_ps[g][:, c0 - lo : c0 - lo + VOC_CHUNK],
+                lhsT=hid_codes[:].bitcast(FP8X4),
+                lhsT_scale=hid_scales[:],
+                rhs=codes[:].bitcast(FP8X4),
+                rhs_scale=scales[:],
+                start=True,
+                stop=True,
+            )
+            if c0 + VOC_CHUNK == hi:
+                nc.vector.tensor_reduce(out=neg_b[:, g : g + 1], in_=b_ps[g][:], axis=AX.X, op=ALU.max, negate=True)
+                nc.scalar.activation(
+                    out=r_sb[g][:], in_=b_ps[g][:], func=ACT.Exp, bias=neg_b[:, g : g + 1], accum_out=r_sum[:, g : g + 1]
+                )
+
+        lm_chunk(0)
+        knn_piece(0)
+        knn_piece(1)
+        lm_chunk(1)
+        lm_chunk(2)
+        knn_piece(2)
+        lm_chunk(3)
+        knn_piece(3)
+
+        p_total = sb.tile([P, 1], F32, name="p_total")
+        nc.vector.tensor_reduce(out=p_total[:], in_=p_sums[:], axis=AX.X, op=ALU.add)
+        p_inv = sb.tile([P, 1], F32, name="p_inv")
+        nc.vector.reciprocal(p_inv[:], p_total[:])
+        p_factor = sb.tile([P, 1], F32, name="p_factor")
+        nc.vector.tensor_scalar(p_factor[:], p_inv[:], lam_sb, 512.0, ALU.mult, ALU.mult)
+
+        neg_all = sb.tile([P, 1], F32, name="neg_all")
+        nc.vector.tensor_reduce(out=neg_all[:], in_=neg_b[:], axis=AX.X, op=ALU.min)
+        rescale = sb.tile([P, len(GROUPS)], F32, name="rescale")
+        nc.scalar.activation(out=rescale[:], in_=neg_b[:], func=ACT.Exp, scale=-1.0, bias=neg_all[:])
+        terms = sb.tile([P, len(GROUPS)], F32, name="terms")
+        r_total = sb.tile([P, 1], F32, name="r_total")
+        nc.vector.scalar_tensor_tensor(
+            out=terms[:], in0=rescale[:], scalar=1.0, in1=r_sum[:], op0=ALU.mult, op1=ALU.mult, accum_out=r_total[:]
+        )
+        r_inv = sb.tile([P, 1], F32, name="r_inv")
+        nc.vector.reciprocal(r_inv[:], r_total[:])
+        r_factor = sb.tile([P, len(GROUPS)], F32, name="r_factor")
+        nc.vector.tensor_scalar(r_factor[:], rescale[:], r_inv[:], lm_share[:], ALU.mult, ALU.mult)
+
+        for g, (lo, hi) in enumerate(GROUPS):
+            knn_part = sb.tile([P, hi - lo], F32, name="knn_part%d" % g)
+            nc.scalar.activation(out=knn_part[:], in_=wf[:, lo:hi], func=ACT.Copy, scale=p_factor[:])
+            mixed = sb.tile([P, hi - lo], F32, name="mixed%d" % g)
+            nc.vector.scalar_tensor_tensor(
+                out=mixed[:], in0=r_sb[g][:], scalar=r_factor[:, g : g + 1], in1=knn_part[:], op0=ALU.mult, op1=ALU.add
+            )
+            nc.sync.dma_start(out=out[:, lo:hi], in_=mixed[:])

@@ -1,6 +1,7 @@
 from contextlib import ExitStack
 
 import concourse.mybir as mybir
+from concourse.masks import make_identity
 
 D, K, T, I, V, Q = 512, 512, 2048, 512, 1024, 128
 FLOPS = 2 * D * Q * I + 2 * K * Q * V
@@ -23,8 +24,7 @@ KN_ROW = 8
 VOC_CHUNK = 256
 GROUPS = ((0, 512), (512, 768), (768, 1024))
 KEY_HALF = 256
-CAST_COLS = 128
-SCATTER_PIECE = 128
+PIECES = ((0, 128), (128, 384), (384, 512))
 
 
 def tile_attend_knnlm_kernel(tc, query, keys_words, keys_scales, kn, hid, voc, lam, offs, offs2, out):
@@ -33,27 +33,29 @@ def tile_attend_knnlm_kernel(tc, query, keys_words, keys_scales, kn, hid, voc, l
         sb = ctx.enter_context(tc.tile_pool(name="sb", bufs=1))
         ps = ctx.enter_context(tc.psum_pool(name="ps", bufs=1))
 
-        def load_rows(flat, rows):
-            raw = flat.rearrange("p (j w) -> p j w", j=PACK)
-            nc.sync.dma_start(out=raw, in_=rows.rearrange("(p j) w -> p j w", j=PACK))
+        def load_rows(name, rows):
+            raw = sb.tile([P, PACK, rows.shape[1]], F32, name=name + "_raw", tag=name + "_raw")
+            nc.sync.dma_start(out=raw[:], in_=rows.rearrange("(p j) w -> p j w", j=PACK))
             return raw
 
-        def cast(name, raw, on_vector=False):
+        def cast(name, raw, copies):
             width = raw.shape[2]
+            step = width // len(copies)
             grouped = sb.tile([P, width, PACK], BF16, name=name + "_bf", align_bytes=64)
-            step = width if on_vector else CAST_COLS
-            for c0 in range(0, width, step):
-                dst = grouped[:, c0 : c0 + step, :].rearrange("p (c i) t -> p c t i", i=4)
-                src = raw[:, :, c0 : c0 + step].rearrange("p t (c i) -> p c t i", i=4)
-                if on_vector:
-                    nc.vector.tensor_copy(out=dst, in_=src)
-                else:
-                    nc.scalar.activation(out=dst, in_=src, func=ACT.Copy)
+            for n, copy in enumerate(copies):
+                c0 = n * step
+                copy(
+                    out=grouped[:, c0 : c0 + step, :].rearrange("p (c i) t -> p c t i", i=4),
+                    in_=raw[:, :, c0 : c0 + step].rearrange("p t (c i) -> p c t i", i=4),
+                )
             return grouped
+
+        def act_copy(out, in_):
+            nc.scalar.activation(out=out, in_=in_, func=ACT.Copy)
 
         def quantize(name, grouped):
             width = grouped.shape[1]
-            codes = sb.tile([P, width], U32, name=name + "_codes", align_bytes=64)
+            codes = sb.tile([P, width], U32, name=name + "_codes", tag=name + "_codes", align_bytes=64)
             scales = sb.tile([P, width], U8, name=name + "_scales", align_bytes=64)
             nc.vector.quantize_mx(
                 out=codes[:].bitcast(FP8X4), scales=scales[:], in_=grouped[:].rearrange("p w t -> p (w t)")
@@ -67,43 +69,43 @@ def tile_attend_knnlm_kernel(tc, query, keys_words, keys_scales, kn, hid, voc, l
         ident = sb.tile([P, P], F32, name="ident")
         key_list = sb.tile([P, I // LANES], U16, name="key_list")
         place_list = sb.tile([P, I // LANES], U16, name="place_list")
-        zeros = sb.tile([P, P], F32, name="zeros", tag="late")
+        lam_sb = sb.tile([P, 1], F32, name="lam_sb")
 
         nc.vector.memset(scale_pool[:].bitcast(I32), 0)
-        nc.vector.memset(kn_pool[:], 0.0)
-        nc.vector.memset(zeros[:], 0.0)
-        nc.vector.memset(wf[:], 0.0)
-        nc.gpsimd.affine_select(
-            out=ident[:], in_=zeros[:], compare_op=ALU.not_equal, fill=1.0, base=0, pattern=[[-1, P]], channel_multiplier=1
-        )
+        nc.vector.memset(kn_pool[:].bitcast(I32), 0)
+        nc.vector.memset(ident[:].bitcast(I32), 0)
+        nc.vector.memset(wf[:].bitcast(I32), 0)
+        nc.gpsimd.dma_start(out=lam_sb[:], in_=lam)
+        make_identity(nc, ident[:], nomemset=True)
 
         nc.sync.dma_start(key_list[:], offs)
-        query_flat = sb.tile([P, PACK * Q], F32, name="query_flat")
-        query_raw = load_rows(query_flat[:], query)
-        nc.scalar.dma_start(out=word_pool[:], in_=keys_words[0].rearrange("p n t -> p (n t)").bitcast(I32))
+        query_raw = load_rows("query", query)
         for quad in range(4):
-            nc.sync.dma_start(
+            queue = nc.sync if quad < 2 else nc.scalar
+            queue.dma_start(
                 out=scale_pool[32 * quad : 32 * quad + 4, :].bitcast(I32),
                 in_=keys_scales[0, 4 * quad : 4 * quad + 4, :].bitcast(I32),
             )
-        nc.sync.dma_start(out=kn_pool[KN_ROW : KN_ROW + 1, :], in_=kn[0:1, :])
-        nc.sync.dma_start(place_list[:], offs2)
+        nc.scalar.dma_start(out=kn_pool[KN_ROW : KN_ROW + 1, :], in_=kn[0:1, :])
+        nc.sync.dma_start(out=word_pool[:], in_=keys_words[0].rearrange("p n t -> p (n t)").bitcast(I32))
+        hid_raw = load_rows("hid", hid)
         n_chunks = V // VOC_CHUNK
-        late = sb.tile([P, PACK * (Q + V) + 8], F32, name="late", tag="late")
-        hid_raw = load_rows(late[:, 0 : PACK * Q], hid)
         voc_raw = []
         for c in range(n_chunks):
-            c0 = c * VOC_CHUNK
-            voc_raw.append(load_rows(late[:, PACK * (Q + c0) : PACK * (Q + c0 + VOC_CHUNK)], voc[:, c0 : c0 + VOC_CHUNK]))
-        lam_sb = late[:, PACK * (Q + V) : PACK * (Q + V) + 1]
-        nc.sync.dma_start(out=lam_sb, in_=lam)
+            voc_raw.append(load_rows("voc%d" % c, voc[:, c * VOC_CHUNK : (c + 1) * VOC_CHUNK]))
+            if c == 1:
+                nc.sync.dma_start(place_list[:], offs2)
+
+        knn_share = sb.tile([P, 1], F32, name="knn_share")
+        lm_share = sb.tile([P, 1], F32, name="lm_share")
+        nc.gpsimd.tensor_scalar(knn_share[:], lam_sb[:], 512.0, 0.0, ALU.mult, ALU.add)
+        nc.gpsimd.tensor_scalar(lm_share[:], lam_sb[:], -512.0, 512.0, ALU.mult, ALU.add)
 
         key_scales = sb.tile([P, I], U8, name="key_scales", align_bytes=64)
         nc.vector.tensor_copy(key_scales[:], scale_pool[:].indirect(key_list[:]))
         kn_listed = sb.tile([P, I], F32, name="kn_listed")
         nc.vector.tensor_copy(kn_listed[:], kn_pool[:].indirect(key_list[:]))
-        query_bf = cast("query", query_raw)
-        query_codes, query_scales = quantize("query", query_bf)
+        query_codes, query_scales = quantize("query", cast("query", query_raw, [nc.scalar.copy]))
 
         kn_turned = ps.tile([P, I // P, P], F32, name="kn_turned")
         for j in range(I // P):
@@ -111,7 +113,7 @@ def tile_attend_knnlm_kernel(tc, query, keys_words, keys_scales, kn, hid, voc, l
         neg_kn = sb.tile([P, I // P], F32, name="neg_kn")
         nc.scalar.activation(out=neg_kn[:], in_=kn_turned[:, :, KN_ROW], func=ACT.Identity, scale=-1.0)
 
-        hid_bf = cast("hid", hid_raw)
+        hid_bf = cast("hid", hid_raw, [act_copy])
         s_ps = ps.tile([P, I], F32, name="s_ps")
         key_words = sb.tile([P, I], I32, name="key_words", tag="kn_then_words", align_bytes=64)
         for h in range(I // KEY_HALF):
@@ -122,8 +124,8 @@ def tile_attend_knnlm_kernel(tc, query, keys_words, keys_scales, kn, hid, voc, l
             )
             a_ps = ps.tile([P, KEY_HALF // P, Q], F32, name="a_ps%d" % h)
             s_turned = sb.tile([P, KEY_HALF // P, Q], F32, name="s_turned%d" % h)
-            for u in range(KEY_HALF // P):
-                j = h * (KEY_HALF // P) + u
+            blocks = range(h * (KEY_HALF // P), (h + 1) * (KEY_HALF // P))
+            for u, j in enumerate(blocks):
                 nc.tensor.matmul_mx(
                     out=a_ps[:, u, :],
                     lhsT=key_words[:, j * P : (j + 1) * P].bitcast(FP8X4),
@@ -133,43 +135,44 @@ def tile_attend_knnlm_kernel(tc, query, keys_words, keys_scales, kn, hid, voc, l
                     start=True,
                     stop=True,
                 )
-            for u in range(KEY_HALF // P):
-                j = h * (KEY_HALF // P) + u
+            for u, j in enumerate(blocks):
                 nc.scalar.activation(
                     out=s_turned[:, u, :], in_=a_ps[:, u, :], func=ACT.Identity, scale=2.0, bias=neg_kn[:, j : j + 1]
                 )
-            for u in range(KEY_HALF // P):
-                j = h * (KEY_HALF // P) + u
+            for u, j in enumerate(blocks):
                 nc.tensor.transpose(s_ps[:, j * P : (j + 1) * P], s_turned[:, u, :], ident[:])
 
         neg_max = sb.tile([P, 1], F32, name="neg_max")
         nc.vector.tensor_reduce(out=neg_max[:], in_=s_ps[:], axis=AX.X, op=ALU.max, negate=True)
-        n_pieces = I // SCATTER_PIECE
-        p_sums = sb.tile([P, n_pieces], F32, name="p_sums")
+        p_sb = sb.tile([P, I], F32, name="p_sb")
+        p_sum = sb.tile([P, 1], F32, name="p_sum")
+        nc.scalar.activation(out=p_sb[:], in_=s_ps[:], func=ACT.Exp, bias=neg_max[:], accum_out=p_sum[:])
+        p_inv = sb.tile([P, 1], F32, name="p_inv")
+        nc.vector.reciprocal(p_inv[:], p_sum[:])
+        p_factor = sb.tile([P, 1], F32, name="p_factor")
+        nc.vector.tensor_tensor(p_factor[:], p_inv[:], knn_share[:], ALU.mult)
 
-        def knn_piece(c):
-            p_sb = sb.tile([P, SCATTER_PIECE], F32, name="p_sb%d" % c)
-            nc.scalar.activation(
-                out=p_sb[:],
-                in_=s_ps[:, c * SCATTER_PIECE : (c + 1) * SCATTER_PIECE],
-                func=ACT.Exp,
-                bias=neg_max[:],
-                accum_out=p_sums[:, c : c + 1],
-            )
-            cols = SCATTER_PIECE // LANES
-            nc.vector.tensor_copy(wf[:].indirect(place_list[:, c * cols : (c + 1) * cols]), p_sb[:])
-
-        lm_share = sb.tile([P, 1], F32, name="lm_share")
-        nc.gpsimd.tensor_scalar(lm_share[:], lam_sb, -512.0, 512.0, ALU.mult, ALU.add)
+        def knn_piece(c, tag, align):
+            lo, hi = PIECES[c]
+            w_sb = sb.tile([P, hi - lo], F32, name="w_sb%d" % c, tag=tag, align_bytes=align)
+            nc.scalar.activation(out=w_sb[:], in_=p_sb[:, lo:hi], func=ACT.Copy, scale=p_factor[:])
+            nc.vector.tensor_copy(wf[:].indirect(place_list[:, lo // LANES : hi // LANES]), w_sb[:])
 
         hid_codes, hid_scales = quantize("hid", hid_bf)
         b_ps = [ps.tile([P, hi - lo], F32, name="b_ps%d" % g) for g, (lo, hi) in enumerate(GROUPS)]
-        neg_b = sb.tile([P, len(GROUPS)], F32, name="neg_b")
-        r_sum = sb.tile([P, len(GROUPS)], F32, name="r_sum")
-        r_sb = [sb.tile([P, hi - lo], F32, name="r_sb%d" % g) for g, (lo, hi) in enumerate(GROUPS)]
+        neg_b = sb.tile([P, V], F32, name="neg_b", tag="neg_b")
+        neg_top = sb.tile([P, len(GROUPS)], F32, name="neg_top")
+
+        voc_copies = [
+            [nc.vector.tensor_copy],
+            [act_copy, nc.vector.tensor_copy],
+            [act_copy, act_copy],
+            [act_copy, act_copy],
+        ]
 
         def lm_chunk(c):
-            codes, scales = quantize("voc%d" % c, cast("voc%d" % c, voc_raw[c], on_vector=(c == 0)))
+            grouped = cast("voc%d" % c, voc_raw[c], voc_copies[c])
+            codes, scales = quantize("voc%d" % c, grouped)
             c0 = c * VOC_CHUNK
             g = [n for n, (lo, hi) in enumerate(GROUPS) if lo <= c0 < hi][0]
             lo, hi = GROUPS[g]
@@ -183,46 +186,37 @@ def tile_attend_knnlm_kernel(tc, query, keys_words, keys_scales, kn, hid, voc, l
                 stop=True,
             )
             if c0 + VOC_CHUNK == hi:
-                nc.vector.tensor_reduce(out=neg_b[:, g : g + 1], in_=b_ps[g][:], axis=AX.X, op=ALU.max, negate=True)
-                nc.scalar.activation(
-                    out=r_sb[g][:], in_=b_ps[g][:], func=ACT.Exp, bias=neg_b[:, g : g + 1], accum_out=r_sum[:, g : g + 1]
+                nc.vector.tensor_scalar(
+                    neg_b[:, lo:hi],
+                    b_ps[g][:],
+                    -1.0,
+                    neg_top[:, g - 1 : g] if g else None,
+                    ALU.mult,
+                    ALU.min,
+                    accum_out=neg_top[:, g : g + 1],
                 )
 
-        lm_chunk(0)
-        knn_piece(0)
-        knn_piece(1)
-        lm_chunk(1)
-        lm_chunk(2)
-        knn_piece(2)
-        lm_chunk(3)
-        knn_piece(3)
+        for c in range(n_chunks):
+            lm_chunk(c)
+        knn_piece(0, "w_sb0", None)
+        knn_piece(1, "voc3_codes", 64)
 
-        p_total = sb.tile([P, 1], F32, name="p_total")
-        nc.vector.tensor_reduce(out=p_total[:], in_=p_sums[:], axis=AX.X, op=ALU.add)
-        p_inv = sb.tile([P, 1], F32, name="p_inv")
-        nc.vector.reciprocal(p_inv[:], p_total[:])
-        p_factor = sb.tile([P, 1], F32, name="p_factor")
-        nc.vector.tensor_scalar(p_factor[:], p_inv[:], lam_sb, 512.0, ALU.mult, ALU.mult)
-
-        neg_all = sb.tile([P, 1], F32, name="neg_all")
-        nc.vector.tensor_reduce(out=neg_all[:], in_=neg_b[:], axis=AX.X, op=ALU.min)
-        rescale = sb.tile([P, len(GROUPS)], F32, name="rescale")
-        nc.scalar.activation(out=rescale[:], in_=neg_b[:], func=ACT.Exp, scale=-1.0, bias=neg_all[:])
-        terms = sb.tile([P, len(GROUPS)], F32, name="terms")
-        r_total = sb.tile([P, 1], F32, name="r_total")
-        nc.vector.scalar_tensor_tensor(
-            out=terms[:], in0=rescale[:], scalar=1.0, in1=r_sum[:], op0=ALU.mult, op1=ALU.mult, accum_out=r_total[:]
+        last = len(GROUPS) - 1
+        r_sb = sb.tile([P, V], F32, name="r_sb")
+        r_sum = sb.tile([P, 1], F32, name="r_sum")
+        nc.scalar.activation(
+            out=r_sb[:], in_=neg_b[:], func=ACT.Exp, scale=-1.0, bias=neg_top[:, last : last + 1], accum_out=r_sum[:]
         )
         r_inv = sb.tile([P, 1], F32, name="r_inv")
-        nc.vector.reciprocal(r_inv[:], r_total[:])
-        r_factor = sb.tile([P, len(GROUPS)], F32, name="r_factor")
-        nc.vector.tensor_scalar(r_factor[:], rescale[:], r_inv[:], lm_share[:], ALU.mult, ALU.mult)
+        nc.vector.reciprocal(r_inv[:], r_sum[:])
+        knn_piece(2, "neg_b", None)
+        r_factor = sb.tile([P, 1], F32, name="r_factor")
+        nc.vector.tensor_tensor(r_factor[:], r_inv[:], lm_share[:], ALU.mult)
 
         for g, (lo, hi) in enumerate(GROUPS):
-            knn_part = sb.tile([P, hi - lo], F32, name="knn_part%d" % g)
-            nc.scalar.activation(out=knn_part[:], in_=wf[:, lo:hi], func=ACT.Copy, scale=p_factor[:])
             mixed = sb.tile([P, hi - lo], F32, name="mixed%d" % g)
             nc.vector.scalar_tensor_tensor(
-                out=mixed[:], in0=r_sb[g][:], scalar=r_factor[:, g : g + 1], in1=knn_part[:], op0=ALU.mult, op1=ALU.add
+                out=mixed[:], in0=r_sb[:, lo:hi], scalar=r_factor[:], in1=wf[:, lo:hi], op0=ALU.mult, op1=ALU.add
             )
-            nc.sync.dma_start(out=out[:, lo:hi], in_=mixed[:])
+            queue = nc.scalar if g == 1 else nc.sync
+            queue.dma_start(out=out[:, lo:hi], in_=mixed[:])

@@ -22,9 +22,9 @@ PACK = 4
 LANES = 16
 KN_ROW = 8
 VOC_CHUNK = 256
-GROUPS = ((0, 512), (512, 768), (768, 1024))
+BANK = 512
 KEY_HALF = 256
-PIECES = ((0, 128), (128, 384), (384, 512))
+OUT_COLS = 256
 
 
 def tile_attend_knnlm_kernel(tc, query, keys_words, keys_scales, kn, hid, voc, lam, offs, offs2, out):
@@ -34,14 +34,14 @@ def tile_attend_knnlm_kernel(tc, query, keys_words, keys_scales, kn, hid, voc, l
         ps = ctx.enter_context(tc.psum_pool(name="ps", bufs=1))
 
         def load_rows(name, rows):
-            raw = sb.tile([P, PACK, rows.shape[1]], F32, name=name + "_raw", tag=name + "_raw")
+            raw = sb.tile([P, PACK, rows.shape[1]], F32, name=name + "_raw", tag=name + "_raw", align_bytes=64)
             nc.sync.dma_start(out=raw[:], in_=rows.rearrange("(p j) w -> p j w", j=PACK))
             return raw
 
         def cast(name, raw, copies):
             width = raw.shape[2]
             step = width // len(copies)
-            grouped = sb.tile([P, width, PACK], BF16, name=name + "_bf", align_bytes=64)
+            grouped = sb.tile([P, width, PACK], BF16, name=name + "_bf", tag=name + "_bf", align_bytes=64)
             for n, copy in enumerate(copies):
                 c0 = n * step
                 copy(
@@ -63,7 +63,7 @@ def tile_attend_knnlm_kernel(tc, query, keys_words, keys_scales, kn, hid, voc, l
             return codes, scales
 
         scale_pool = sb.tile([P, T], U8, name="scale_pool", align_bytes=64)
-        kn_pool = sb.tile([P, T], F32, name="kn_pool", tag="kn_then_words", align_bytes=64)
+        kn_pool = sb.tile([P, T], F32, name="kn_pool")
         word_pool = sb.tile([P, T], I32, name="word_pool")
         wf = sb.tile([P, V], F32, name="wf")
         ident = sb.tile([P, P], F32, name="ident")
@@ -71,59 +71,61 @@ def tile_attend_knnlm_kernel(tc, query, keys_words, keys_scales, kn, hid, voc, l
         place_list = sb.tile([P, I // LANES], U16, name="place_list")
         lam_sb = sb.tile([P, 1], F32, name="lam_sb")
 
-        nc.vector.memset(scale_pool[:].bitcast(I32), 0)
         nc.vector.memset(kn_pool[:].bitcast(I32), 0)
+        nc.vector.memset(scale_pool[:].bitcast(I32), 0)
         nc.vector.memset(ident[:].bitcast(I32), 0)
         nc.vector.memset(wf[:].bitcast(I32), 0)
         nc.gpsimd.dma_start(out=lam_sb[:], in_=lam)
         make_identity(nc, ident[:], nomemset=True)
 
         nc.sync.dma_start(key_list[:], offs)
-        query_raw = load_rows("query", query)
+        nc.sync.dma_start(out=word_pool[:], in_=keys_words[0].rearrange("p n t -> p (n t)").bitcast(I32))
+        nc.sync.dma_start(out=kn_pool[KN_ROW : KN_ROW + 1, :], in_=kn[0:1, :])
         for quad in range(4):
-            queue = nc.sync if quad < 2 else nc.scalar
-            queue.dma_start(
+            nc.sync.dma_start(
                 out=scale_pool[32 * quad : 32 * quad + 4, :].bitcast(I32),
                 in_=keys_scales[0, 4 * quad : 4 * quad + 4, :].bitcast(I32),
             )
-        nc.scalar.dma_start(out=kn_pool[KN_ROW : KN_ROW + 1, :], in_=kn[0:1, :])
-        nc.sync.dma_start(out=word_pool[:], in_=keys_words[0].rearrange("p n t -> p (n t)").bitcast(I32))
-        hid_raw = load_rows("hid", hid)
+        query_raw = load_rows("query", query)
         n_chunks = V // VOC_CHUNK
-        voc_raw = []
-        for c in range(n_chunks):
+        voc_raw = [load_rows("voc0", voc[:, 0:VOC_CHUNK])]
+        hid_raw = load_rows("hid", hid)
+        for c in range(1, n_chunks):
             voc_raw.append(load_rows("voc%d" % c, voc[:, c * VOC_CHUNK : (c + 1) * VOC_CHUNK]))
-            if c == 1:
-                nc.sync.dma_start(place_list[:], offs2)
+        nc.sync.dma_start(place_list[:], offs2)
 
         knn_share = sb.tile([P, 1], F32, name="knn_share")
         lm_share = sb.tile([P, 1], F32, name="lm_share")
         nc.gpsimd.tensor_scalar(knn_share[:], lam_sb[:], 512.0, 0.0, ALU.mult, ALU.add)
         nc.gpsimd.tensor_scalar(lm_share[:], lam_sb[:], -512.0, 512.0, ALU.mult, ALU.add)
 
-        key_scales = sb.tile([P, I], U8, name="key_scales", align_bytes=64)
-        nc.vector.tensor_copy(key_scales[:], scale_pool[:].indirect(key_list[:]))
+        key_words = sb.tile([P, I], I32, name="key_words", align_bytes=64)
+        nc.vector.tensor_copy(key_words[:].bitcast(U32), word_pool[:].bitcast(U32).indirect(key_list[:]))
         kn_listed = sb.tile([P, I], F32, name="kn_listed")
         nc.vector.tensor_copy(kn_listed[:], kn_pool[:].indirect(key_list[:]))
-        query_codes, query_scales = quantize("query", cast("query", query_raw, [nc.scalar.copy]))
+        query_codes, query_scales = quantize("query", cast("query", query_raw, [act_copy]))
+        key_scales = sb.tile([P, I], U8, name="key_scales", tag="query_raw", align_bytes=64)
+        for lo in range(0, I, KEY_HALF):
+            hi = lo + KEY_HALF
+            nc.vector.tensor_copy(key_scales[:, lo:hi], scale_pool[:].indirect(key_list[:, lo // LANES : hi // LANES]))
 
+        def voc_chunk(c):
+            copies = [[act_copy, act_copy], [nc.vector.tensor_copy], [act_copy, act_copy], [act_copy, nc.vector.tensor_copy]][c]
+            return quantize("voc%d" % c, cast("voc%d" % c, voc_raw[c], copies))
+
+        voc_mx = [voc_chunk(0)]
         kn_turned = ps.tile([P, I // P, P], F32, name="kn_turned")
         for j in range(I // P):
             nc.tensor.transpose(kn_turned[:, j, :], kn_listed[:, j * P : (j + 1) * P], ident[:])
-        neg_kn = sb.tile([P, I // P], F32, name="neg_kn")
+        neg_kn = sb.tile([P, I // P], F32, name="neg_kn", tag="voc0_raw", align_bytes=64)
         nc.scalar.activation(out=neg_kn[:], in_=kn_turned[:, :, KN_ROW], func=ACT.Identity, scale=-1.0)
+        hid_codes, hid_scales = quantize("hid", cast("hid", hid_raw, [act_copy]))
+        voc_mx.append(voc_chunk(1))
 
-        hid_bf = cast("hid", hid_raw, [act_copy])
         s_ps = ps.tile([P, I], F32, name="s_ps")
-        key_words = sb.tile([P, I], I32, name="key_words", tag="kn_then_words", align_bytes=64)
+        s_turned = sb.tile([P, I // P, Q], F32, name="s_turned", tag="hid_raw", align_bytes=64)
         for h in range(I // KEY_HALF):
-            cols = KEY_HALF // LANES
-            nc.vector.tensor_copy(
-                key_words[:, h * KEY_HALF : (h + 1) * KEY_HALF].bitcast(U32),
-                word_pool[:].bitcast(U32).indirect(key_list[:, h * cols : (h + 1) * cols]),
-            )
             a_ps = ps.tile([P, KEY_HALF // P, Q], F32, name="a_ps%d" % h)
-            s_turned = sb.tile([P, KEY_HALF // P, Q], F32, name="s_turned%d" % h)
             blocks = range(h * (KEY_HALF // P), (h + 1) * (KEY_HALF // P))
             for u, j in enumerate(blocks):
                 nc.tensor.matmul_mx(
@@ -137,47 +139,26 @@ def tile_attend_knnlm_kernel(tc, query, keys_words, keys_scales, kn, hid, voc, l
                 )
             for u, j in enumerate(blocks):
                 nc.scalar.activation(
-                    out=s_turned[:, u, :], in_=a_ps[:, u, :], func=ACT.Identity, scale=2.0, bias=neg_kn[:, j : j + 1]
+                    out=s_turned[:, j, :], in_=a_ps[:, u, :], func=ACT.Identity, scale=2.0, bias=neg_kn[:, j : j + 1]
                 )
             for u, j in enumerate(blocks):
-                nc.tensor.transpose(s_ps[:, j * P : (j + 1) * P], s_turned[:, u, :], ident[:])
+                nc.tensor.transpose(s_ps[:, j * P : (j + 1) * P], s_turned[:, j, :], ident[:])
 
-        neg_max = sb.tile([P, 1], F32, name="neg_max")
+        neg_max = sb.tile([P, 1], F32, name="neg_max", tag="voc1_bf", align_bytes=64)
         nc.vector.tensor_reduce(out=neg_max[:], in_=s_ps[:], axis=AX.X, op=ALU.max, negate=True)
-        p_sb = sb.tile([P, I], F32, name="p_sb")
+        for c in range(2, n_chunks):
+            voc_mx.append(voc_chunk(c))
+        p_sb = sb.tile([P, I], F32, name="p_sb", tag="voc2_bf", align_bytes=64)
         p_sum = sb.tile([P, 1], F32, name="p_sum")
         nc.scalar.activation(out=p_sb[:], in_=s_ps[:], func=ACT.Exp, bias=neg_max[:], accum_out=p_sum[:])
         p_inv = sb.tile([P, 1], F32, name="p_inv")
         nc.vector.reciprocal(p_inv[:], p_sum[:])
-        p_factor = sb.tile([P, 1], F32, name="p_factor")
-        nc.vector.tensor_tensor(p_factor[:], p_inv[:], knn_share[:], ALU.mult)
 
-        def knn_piece(c, tag, align):
-            lo, hi = PIECES[c]
-            w_sb = sb.tile([P, hi - lo], F32, name="w_sb%d" % c, tag=tag, align_bytes=align)
-            nc.scalar.activation(out=w_sb[:], in_=p_sb[:, lo:hi], func=ACT.Copy, scale=p_factor[:])
-            nc.vector.tensor_copy(wf[:].indirect(place_list[:, lo // LANES : hi // LANES]), w_sb[:])
-
-        hid_codes, hid_scales = quantize("hid", hid_bf)
-        b_ps = [ps.tile([P, hi - lo], F32, name="b_ps%d" % g) for g, (lo, hi) in enumerate(GROUPS)]
-        neg_b = sb.tile([P, V], F32, name="neg_b", tag="neg_b")
-        neg_top = sb.tile([P, len(GROUPS)], F32, name="neg_top")
-
-        voc_copies = [
-            [nc.vector.tensor_copy],
-            [act_copy, nc.vector.tensor_copy],
-            [act_copy, act_copy],
-            [act_copy, act_copy],
-        ]
-
-        def lm_chunk(c):
-            grouped = cast("voc%d" % c, voc_raw[c], voc_copies[c])
-            codes, scales = quantize("voc%d" % c, grouped)
-            c0 = c * VOC_CHUNK
-            g = [n for n, (lo, hi) in enumerate(GROUPS) if lo <= c0 < hi][0]
-            lo, hi = GROUPS[g]
+        b_ps = [ps.tile([P, BANK], F32, name="b_ps%d" % g) for g in range(V // BANK)]
+        for c, (codes, scales) in enumerate(voc_mx):
+            g, c0 = divmod(c * VOC_CHUNK, BANK)
             nc.tensor.matmul_mx(
-                out=b_ps[g][:, c0 - lo : c0 - lo + VOC_CHUNK],
+                out=b_ps[g][:, c0 : c0 + VOC_CHUNK],
                 lhsT=hid_codes[:].bitcast(FP8X4),
                 lhsT_scale=hid_scales[:],
                 rhs=codes[:].bitcast(FP8X4),
@@ -185,38 +166,29 @@ def tile_attend_knnlm_kernel(tc, query, keys_words, keys_scales, kn, hid, voc, l
                 start=True,
                 stop=True,
             )
-            if c0 + VOC_CHUNK == hi:
-                nc.vector.tensor_scalar(
-                    neg_b[:, lo:hi],
-                    b_ps[g][:],
-                    -1.0,
-                    neg_top[:, g - 1 : g] if g else None,
-                    ALU.mult,
-                    ALU.min,
-                    accum_out=neg_top[:, g : g + 1],
-                )
 
-        for c in range(n_chunks):
-            lm_chunk(c)
-        knn_piece(0, "w_sb0", None)
-        knn_piece(1, "voc3_codes", 64)
+        neg_b = sb.tile([P, V], F32, name="neg_b")
+        neg_top0 = sb.tile([P, 1], F32, name="neg_top0", tag="voc3_raw", align_bytes=64)
+        neg_top = sb.tile([P, 1], F32, name="neg_top")
+        nc.vector.tensor_scalar(neg_b[:, 0:BANK], b_ps[0][:], -1.0, None, ALU.mult, ALU.min, accum_out=neg_top0[:])
+        w_sb = sb.tile([P, I], F32, name="w_sb", tag="voc3_codes", align_bytes=64)
+        nc.vector.tensor_scalar(w_sb[:], p_sb[:], p_inv[:], knn_share[:], ALU.mult, ALU.mult)
+        nc.vector.tensor_scalar(neg_b[:, BANK:V], b_ps[1][:], -1.0, neg_top0[:], ALU.mult, ALU.min, accum_out=neg_top[:])
+        nc.vector.tensor_copy(wf[:].indirect(place_list[:]), w_sb[:])
 
-        last = len(GROUPS) - 1
         r_sb = sb.tile([P, V], F32, name="r_sb")
         r_sum = sb.tile([P, 1], F32, name="r_sum")
-        nc.scalar.activation(
-            out=r_sb[:], in_=neg_b[:], func=ACT.Exp, scale=-1.0, bias=neg_top[:, last : last + 1], accum_out=r_sum[:]
-        )
+        nc.scalar.activation(out=r_sb[:], in_=neg_b[:], func=ACT.Exp, scale=-1.0, bias=neg_top[:], accum_out=r_sum[:])
+        r_share = sb.tile([P, V], F32, name="r_share")
+        nc.scalar.activation(out=r_share[:], in_=r_sb[:], func=ACT.Copy, scale=lm_share[:])
         r_inv = sb.tile([P, 1], F32, name="r_inv")
         nc.vector.reciprocal(r_inv[:], r_sum[:])
-        knn_piece(2, "neg_b", None)
-        r_factor = sb.tile([P, 1], F32, name="r_factor")
-        nc.vector.tensor_tensor(r_factor[:], r_inv[:], lm_share[:], ALU.mult)
 
-        for g, (lo, hi) in enumerate(GROUPS):
+        for g, lo in enumerate(range(0, V, OUT_COLS)):
+            hi = lo + OUT_COLS
             mixed = sb.tile([P, hi - lo], F32, name="mixed%d" % g)
             nc.vector.scalar_tensor_tensor(
-                out=mixed[:], in0=r_sb[:, lo:hi], scalar=r_factor[:], in1=wf[:, lo:hi], op0=ALU.mult, op1=ALU.add
+                out=mixed[:], in0=r_share[:, lo:hi], scalar=r_inv[:], in1=wf[:, lo:hi], op0=ALU.mult, op1=ALU.add
             )
-            queue = nc.scalar if g == 1 else nc.sync
+            queue = nc.scalar if g % 2 else nc.sync
             queue.dma_start(out=out[:, lo:hi], in_=mixed[:])

@@ -1,7 +1,6 @@
 from contextlib import ExitStack
 
 import concourse.mybir as mybir
-from concourse.masks import make_identity
 
 D, K, T, I, V, Q = 512, 512, 2048, 512, 1024, 128
 FLOPS = 2 * D * Q * I + 2 * K * Q * V
@@ -20,10 +19,12 @@ AX = mybir.AxisListType
 P = 128
 PACK = 4
 LANES = 16
-KN_ROW = 8
-VOC_CHUNK = 256
-BANK = 512
-KEY_HALF = 256
+KN_ROW = P - 1
+CHUNK = 256
+N_CHUNKS = V // CHUNK
+EARLY = V - CHUNK
+HALF = I // 2
+PIECE = 128
 OUT_COLS = 256
 
 
@@ -33,162 +34,210 @@ def tile_attend_knnlm_kernel(tc, query, keys_words, keys_scales, kn, hid, voc, l
         sb = ctx.enter_context(tc.tile_pool(name="sb", bufs=1))
         ps = ctx.enter_context(tc.psum_pool(name="ps", bufs=1))
 
+        def tile(name, shape, dtype, tag=None):
+            return sb.tile(shape, dtype, name=name, tag=tag or name, align_bytes=64)
+
         def load_rows(name, rows):
-            raw = sb.tile([P, PACK, rows.shape[1]], F32, name=name + "_raw", tag=name + "_raw", align_bytes=64)
+            raw = tile(name + "_raw", [P, PACK, rows.shape[1]], F32)
             nc.sync.dma_start(out=raw[:], in_=rows.rearrange("(p j) w -> p j w", j=PACK))
             return raw
-
-        def cast(name, raw, copies):
-            width = raw.shape[2]
-            step = width // len(copies)
-            grouped = sb.tile([P, width, PACK], BF16, name=name + "_bf", tag=name + "_bf", align_bytes=64)
-            for n, copy in enumerate(copies):
-                c0 = n * step
-                copy(
-                    out=grouped[:, c0 : c0 + step, :].rearrange("p (c i) t -> p c t i", i=4),
-                    in_=raw[:, :, c0 : c0 + step].rearrange("p t (c i) -> p c t i", i=4),
-                )
-            return grouped
 
         def act_copy(out, in_):
             nc.scalar.activation(out=out, in_=in_, func=ACT.Copy)
 
+        def interleave(copy, grouped, raw):
+            copy(
+                out=grouped.rearrange("p (c i) t -> p c t i", i=4),
+                in_=raw.rearrange("p t (c i) -> p c t i", i=4),
+            )
+
+        def cast(name, raw):
+            grouped = tile(name + "_bf", [P, raw.shape[2], PACK], BF16)
+            interleave(act_copy, grouped[:], raw[:])
+            return grouped
+
         def quantize(name, grouped):
             width = grouped.shape[1]
-            codes = sb.tile([P, width], U32, name=name + "_codes", tag=name + "_codes", align_bytes=64)
-            scales = sb.tile([P, width], U8, name=name + "_scales", align_bytes=64)
+            codes = tile(name + "_codes", [P, width], U32)
+            scales = tile(name + "_scales", [P, width], U8)
             nc.vector.quantize_mx(
                 out=codes[:].bitcast(FP8X4), scales=scales[:], in_=grouped[:].rearrange("p w t -> p (w t)")
             )
             return codes, scales
 
-        scale_pool = sb.tile([P, T], U8, name="scale_pool", align_bytes=64)
-        kn_pool = sb.tile([P, T], F32, name="kn_pool")
-        word_pool = sb.tile([P, T], I32, name="word_pool")
-        wf = sb.tile([P, V], F32, name="wf")
-        ident = sb.tile([P, P], F32, name="ident")
-        key_list = sb.tile([P, I // LANES], U16, name="key_list")
-        place_list = sb.tile([P, I // LANES], U16, name="place_list")
-        lam_sb = sb.tile([P, 1], F32, name="lam_sb")
-
-        nc.vector.memset(kn_pool[:].bitcast(I32), 0)
-        nc.vector.memset(scale_pool[:].bitcast(I32), 0)
-        nc.vector.memset(ident[:].bitcast(I32), 0)
-        nc.vector.memset(wf[:].bitcast(I32), 0)
-        nc.gpsimd.dma_start(out=lam_sb[:], in_=lam)
-        make_identity(nc, ident[:], nomemset=True)
-
-        nc.sync.dma_start(key_list[:], offs)
-        nc.sync.dma_start(out=word_pool[:], in_=keys_words[0].rearrange("p n t -> p (n t)").bitcast(I32))
-        nc.sync.dma_start(out=kn_pool[KN_ROW : KN_ROW + 1, :], in_=kn[0:1, :])
-        for quad in range(4):
-            nc.sync.dma_start(
-                out=scale_pool[32 * quad : 32 * quad + 4, :].bitcast(I32),
-                in_=keys_scales[0, 4 * quad : 4 * quad + 4, :].bitcast(I32),
-            )
-        query_raw = load_rows("query", query)
-        n_chunks = V // VOC_CHUNK
-        voc_raw = [load_rows("voc0", voc[:, 0:VOC_CHUNK])]
-        hid_raw = load_rows("hid", hid)
-        for c in range(1, n_chunks):
-            voc_raw.append(load_rows("voc%d" % c, voc[:, c * VOC_CHUNK : (c + 1) * VOC_CHUNK]))
-        nc.sync.dma_start(place_list[:], offs2)
-
-        knn_share = sb.tile([P, 1], F32, name="knn_share")
-        lm_share = sb.tile([P, 1], F32, name="lm_share")
-        nc.gpsimd.tensor_scalar(knn_share[:], lam_sb[:], 512.0, 0.0, ALU.mult, ALU.add)
-        nc.gpsimd.tensor_scalar(lm_share[:], lam_sb[:], -512.0, 512.0, ALU.mult, ALU.add)
-
-        key_words = sb.tile([P, I], I32, name="key_words", align_bytes=64)
-        nc.vector.tensor_copy(key_words[:].bitcast(U32), word_pool[:].bitcast(U32).indirect(key_list[:]))
-        kn_listed = sb.tile([P, I], F32, name="kn_listed")
-        nc.vector.tensor_copy(kn_listed[:], kn_pool[:].indirect(key_list[:]))
-        query_codes, query_scales = quantize("query", cast("query", query_raw, [act_copy]))
-        key_scales = sb.tile([P, I], U8, name="key_scales", tag="query_raw", align_bytes=64)
-        for lo in range(0, I, KEY_HALF):
-            hi = lo + KEY_HALF
-            nc.vector.tensor_copy(key_scales[:, lo:hi], scale_pool[:].indirect(key_list[:, lo // LANES : hi // LANES]))
-
-        def voc_chunk(c):
-            copies = [[act_copy, act_copy], [nc.vector.tensor_copy], [act_copy, act_copy], [act_copy, nc.vector.tensor_copy]][c]
-            return quantize("voc%d" % c, cast("voc%d" % c, voc_raw[c], copies))
-
-        voc_mx = [voc_chunk(0)]
-        kn_turned = ps.tile([P, I // P, P], F32, name="kn_turned")
-        for j in range(I // P):
-            nc.tensor.transpose(kn_turned[:, j, :], kn_listed[:, j * P : (j + 1) * P], ident[:])
-        neg_kn = sb.tile([P, I // P], F32, name="neg_kn", tag="voc0_raw", align_bytes=64)
-        nc.scalar.activation(out=neg_kn[:], in_=kn_turned[:, :, KN_ROW], func=ACT.Identity, scale=-1.0)
-        hid_codes, hid_scales = quantize("hid", cast("hid", hid_raw, [act_copy]))
-        voc_mx.append(voc_chunk(1))
-
-        s_ps = ps.tile([P, I], F32, name="s_ps")
-        s_turned = sb.tile([P, I // P, Q], F32, name="s_turned", tag="hid_raw", align_bytes=64)
-        for h in range(I // KEY_HALF):
-            a_ps = ps.tile([P, KEY_HALF // P, Q], F32, name="a_ps%d" % h)
-            blocks = range(h * (KEY_HALF // P), (h + 1) * (KEY_HALF // P))
-            for u, j in enumerate(blocks):
-                nc.tensor.matmul_mx(
-                    out=a_ps[:, u, :],
-                    lhsT=key_words[:, j * P : (j + 1) * P].bitcast(FP8X4),
-                    lhsT_scale=key_scales[:, j * P : (j + 1) * P],
-                    rhs=query_codes[:].bitcast(FP8X4),
-                    rhs_scale=query_scales[:],
-                    start=True,
-                    stop=True,
-                )
-            for u, j in enumerate(blocks):
-                nc.scalar.activation(
-                    out=s_turned[:, j, :], in_=a_ps[:, u, :], func=ACT.Identity, scale=2.0, bias=neg_kn[:, j : j + 1]
-                )
-            for u, j in enumerate(blocks):
-                nc.tensor.transpose(s_ps[:, j * P : (j + 1) * P], s_turned[:, j, :], ident[:])
-
-        neg_max = sb.tile([P, 1], F32, name="neg_max", tag="voc1_bf", align_bytes=64)
-        nc.vector.tensor_reduce(out=neg_max[:], in_=s_ps[:], axis=AX.X, op=ALU.max, negate=True)
-        for c in range(2, n_chunks):
-            voc_mx.append(voc_chunk(c))
-        p_sb = sb.tile([P, I], F32, name="p_sb", tag="voc2_bf", align_bytes=64)
-        p_sum = sb.tile([P, 1], F32, name="p_sum")
-        nc.scalar.activation(out=p_sb[:], in_=s_ps[:], func=ACT.Exp, bias=neg_max[:], accum_out=p_sum[:])
-        p_inv = sb.tile([P, 1], F32, name="p_inv")
-        nc.vector.reciprocal(p_inv[:], p_sum[:])
-
-        b_ps = [ps.tile([P, BANK], F32, name="b_ps%d" % g) for g in range(V // BANK)]
-        for c, (codes, scales) in enumerate(voc_mx):
-            g, c0 = divmod(c * VOC_CHUNK, BANK)
+        def product(out_ps, stationary, moving):
             nc.tensor.matmul_mx(
-                out=b_ps[g][:, c0 : c0 + VOC_CHUNK],
-                lhsT=hid_codes[:].bitcast(FP8X4),
-                lhsT_scale=hid_scales[:],
-                rhs=codes[:].bitcast(FP8X4),
-                rhs_scale=scales[:],
+                out=out_ps,
+                lhsT=stationary[0].bitcast(FP8X4),
+                lhsT_scale=stationary[1],
+                rhs=moving[0].bitcast(FP8X4),
+                rhs_scale=moving[1],
                 start=True,
                 stop=True,
             )
 
-        neg_b = sb.tile([P, V], F32, name="neg_b")
-        neg_top0 = sb.tile([P, 1], F32, name="neg_top0", tag="voc3_raw", align_bytes=64)
-        neg_top = sb.tile([P, 1], F32, name="neg_top")
-        nc.vector.tensor_scalar(neg_b[:, 0:BANK], b_ps[0][:], -1.0, None, ALU.mult, ALU.min, accum_out=neg_top0[:])
-        w_sb = sb.tile([P, I], F32, name="w_sb", tag="voc3_codes", align_bytes=64)
-        nc.vector.tensor_scalar(w_sb[:], p_sb[:], p_inv[:], knn_share[:], ALU.mult, ALU.mult)
-        nc.vector.tensor_scalar(neg_b[:, BANK:V], b_ps[1][:], -1.0, neg_top0[:], ALU.mult, ALU.min, accum_out=neg_top[:])
-        nc.vector.tensor_copy(wf[:].indirect(place_list[:]), w_sb[:])
+        scale_pool = tile("scale_pool", [P, T], U8)
+        kn_pool = tile("kn_pool", [P, T], F32)
+        word_pool = tile("word_pool", [P, T], I32)
+        ident = tile("ident", [P, P], F32)
+        key_list = tile("key_list", [P, I // LANES], U16)
+        place_list = tile("place_list", [P, I // LANES], U16)
+        lam_sb = tile("lam_sb", [P, 1], F32)
 
-        r_sb = sb.tile([P, V], F32, name="r_sb")
-        r_sum = sb.tile([P, 1], F32, name="r_sum")
-        nc.scalar.activation(out=r_sb[:], in_=neg_b[:], func=ACT.Exp, scale=-1.0, bias=neg_top[:], accum_out=r_sum[:])
-        r_share = sb.tile([P, V], F32, name="r_share")
-        nc.scalar.activation(out=r_share[:], in_=r_sb[:], func=ACT.Copy, scale=lm_share[:])
-        r_inv = sb.tile([P, 1], F32, name="r_inv")
+        nc.gpsimd.memset(scale_pool[:].bitcast(I32), 0)
+        nc.vector.memset(kn_pool[0:KN_ROW, :].bitcast(I32), 0)
+        zeros = tile("zeros", [P, P], F32, tag="wf")
+        nc.gpsimd.memset(zeros[:], 0.0)
+        nc.gpsimd.affine_select(
+            out=ident[:], in_=zeros[:], compare_op=ALU.not_equal, fill=1.0, base=0, pattern=[[-1, P]], channel_multiplier=1
+        )
+        wf = tile("wf", [P, V], F32)
+        nc.gpsimd.memset(wf[:].bitcast(I32), 0)
+        nc.gpsimd.dma_start(out=lam_sb[:], in_=lam)
+
+        nc.sync.dma_start(key_list[:], offs)
+        nc.sync.dma_start(out=kn_pool[KN_ROW:P, :], in_=kn[0:1, :])
+        query_raw = load_rows("query", query)
+        for row in range(4):
+            nc.sync.dma_start(
+                out=scale_pool[row:P:32, :].bitcast(I32), in_=keys_scales[0, row:16:4, :].bitcast(I32)
+            )
+        nc.sync.dma_start(out=word_pool[:], in_=keys_words[0].rearrange("p n t -> p (n t)").bitcast(I32))
+        hid_raw = load_rows("hid", hid)
+        voc_raw = [load_rows("voc0", voc[:, 0:CHUNK])]
+        nc.sync.dma_start(place_list[:], offs2)
+        for c in range(1, N_CHUNKS):
+            voc_raw.append(load_rows("voc%d" % c, voc[:, c * CHUNK : (c + 1) * CHUNK]))
+
+        kn_listed = tile("kn_listed", [P, I], F32)
+        nc.vector.tensor_copy(kn_listed[:], kn_pool[:].indirect(key_list[:]))
+        key_scales = tile("key_scales", [P, I], U8)
+        nc.vector.tensor_copy(key_scales[:], scale_pool[:].indirect(key_list[:]))
+        query_codes, query_scales = quantize("query", cast("query", query_raw))
+        kn_turned = ps.tile([P, I // P, P], F32, name="kn_turned")
+        for j in range(I // P):
+            nc.tensor.transpose(kn_turned[:, j, :], kn_listed[:, j * P : (j + 1) * P], ident[:])
+        neg_kn = tile("neg_kn", [P, I // P], F32)
+        nc.scalar.activation(out=neg_kn[:], in_=kn_turned[:, :, KN_ROW], func=ACT.Copy, scale=-1.0)
+
+        s_ps = ps.tile([P, I], F32, name="s_ps")
+        for h in range(2):
+            lo = h * HALF
+            key_words = tile("key_words%d" % h, [P, HALF], I32)
+            nc.vector.tensor_copy(
+                key_words[:].bitcast(U32),
+                word_pool[:].bitcast(U32).indirect(key_list[:, lo // LANES : (lo + HALF) // LANES]),
+            )
+            a_ps = ps.tile([P, HALF // P, Q], F32, name="a_ps%d" % h)
+            s_turned = tile("s_turned%d" % h, [P, HALF // P, Q], F32)
+            for u in range(HALF // P):
+                keys = (key_words[:, u * P : (u + 1) * P], key_scales[:, lo + u * P : lo + (u + 1) * P])
+                product(a_ps[:, u, :], keys, (query_codes[:], query_scales[:]))
+            for u in range(HALF // P):
+                j = lo // P + u
+                nc.scalar.activation(
+                    out=s_turned[:, u, :], in_=a_ps[:, u, :], func=ACT.Identity, scale=2.0, bias=neg_kn[:, j : j + 1]
+                )
+            for u in range(HALF // P):
+                nc.tensor.transpose(s_ps[:, lo + u * P : lo + (u + 1) * P], s_turned[:, u, :], ident[:])
+
+        hid_codes, hid_scales = quantize("hid", cast("hid", hid_raw))
+        neg_early = tile("neg_early", [P, EARLY], F32)
+        neg_last = tile("neg_last", [P, CHUNK], F32)
+        grouped = {c: tile("voc%d_bf" % c, [P, CHUNK, PACK], BF16) for c in (0, 1, 3)}
+        b_ps = [ps.tile([P, CHUNK], F32, name="b_ps%d" % c) for c in range(N_CHUNKS)]
+        lows = []
+
+        def cast_cols(c, lo, hi, copy):
+            interleave(copy, grouped[c][:, lo:hi, :], voc_raw[c][:, :, lo:hi])
+
+        def multiply(c):
+            codes, scales = quantize("voc%d" % c, grouped[c])
+            product(b_ps[c][:], (hid_codes[:], hid_scales[:]), (codes[:], scales[:]))
+
+        def lowest(c):
+            dst = neg_last[:] if c == N_CHUNKS - 1 else neg_early[:, c * CHUNK : (c + 1) * CHUNK]
+            low = tile("low%d" % c, [P, 1], F32)
+            start = lows[-1][:] if lows else None
+            nc.vector.tensor_scalar(dst, b_ps[c][:], -1.0, start, ALU.mult, ALU.min, accum_out=low[:])
+            lows.append(low)
+
+        def scatter(lo, w):
+            hi = lo + w.shape[1]
+            nc.vector.tensor_copy(wf[:].indirect(place_list[:, lo // LANES : hi // LANES]), w[:])
+
+        def weights(n, tag):
+            w = tile("w%d" % n, [P, PIECE], F32, tag=tag)
+            nc.scalar.activation(out=w[:], in_=p_sb[:, n * PIECE : (n + 1) * PIECE], func=ACT.Copy, scale=w_factor[:])
+            return w
+
+        knn_share = tile("knn_share", [P, 1], F32)
+        shares = tile("shares", [P, 2], F32)
+        nc.gpsimd.tensor_scalar(knn_share[:], lam_sb[:], 512.0, 0.0, ALU.mult, ALU.add)
+        nc.gpsimd.tensor_scalar(shares[:, 1:2], lam_sb[:], -512.0, 512.0, ALU.mult, ALU.add)
+
+        cast_cols(0, 0, CHUNK, nc.vector.tensor_copy)
+        multiply(0)
+        neg_max = tile("neg_max", [P, 1], F32, tag="voc0_raw")
+        nc.vector.tensor_reduce(out=neg_max[:], in_=s_ps[:], axis=AX.X, op=ALU.max, negate=True)
+        lowest(0)
+        cast_cols(1, 0, CHUNK, act_copy)
+        p_sb = tile("p_sb", [P, I], F32, tag="voc1_raw")
+        p_sum = tile("p_sum", [P, 1], F32)
+        nc.scalar.activation(out=p_sb[:], in_=s_ps[:], func=ACT.Exp, bias=neg_max[:], accum_out=p_sum[:])
+        multiply(1)
+        grouped.setdefault(2, tile("voc2_bf", [P, CHUNK, PACK], BF16, tag="voc0_raw"))
+        cast_cols(2, 0, CHUNK // 2, nc.vector.tensor_copy)
+        cast_cols(2, CHUNK // 2, CHUNK, act_copy)
+        p_inv = tile("p_inv", [P, 1], F32)
+        nc.vector.reciprocal(p_inv[:], p_sum[:])
+        lowest(1)
+        w_first = tile("w_first", [P, PIECE], F32)
+        nc.vector.tensor_scalar(w_first[:], p_sb[:, 0:PIECE], p_inv[:], knn_share[:], ALU.mult, ALU.mult)
+        w_factor = tile("w_factor", [P, 1], F32)
+        nc.vector.tensor_scalar(w_factor[:], p_inv[:], knn_share[:], None, ALU.mult)
+        multiply(2)
+        scatter(0, w_first)
+        lowest(2)
+        cast_cols(3, 0, CHUNK, act_copy)
+        multiply(3)
+        scatter(PIECE, weights(1, "voc3_raw"))
+
+        r_sb = tile("r_sb", [P, V], F32)
+        sum_early = tile("sum_early", [P, 1], F32)
+        sum_last = tile("sum_last", [P, 1], F32)
+        low_early = lows[-1]
+        nc.scalar.activation(
+            out=r_sb[:, 0:EARLY], in_=neg_early[:], func=ACT.Exp, scale=-1.0, bias=low_early[:], accum_out=sum_early[:]
+        )
+        lowest(3)
+        low_last = lows[-1]
+        scatter(2 * PIECE, weights(2, "voc3_codes"))
+        shrink = tile("shrink", [P, 1], F32)
+        nc.scalar.activation(out=shrink[:], in_=low_early[:], func=ACT.Exp, scale=-1.0, bias=low_last[:])
+        nc.scalar.activation(
+            out=r_sb[:, EARLY:V], in_=neg_last[:], func=ACT.Exp, scale=-1.0, bias=low_last[:], accum_out=sum_last[:]
+        )
+        nc.scalar.activation(out=shares[:, 0:1], in_=shares[:, 1:2], func=ACT.Copy, scale=shrink[:])
+        r_sum = tile("r_sum", [P, 1], F32)
+        nc.scalar.activation(out=r_sum[:], in_=sum_early[:], func=ACT.Identity, scale=shrink[:], bias=sum_last[:])
+        r_inv = tile("r_inv", [P, 1], F32)
         nc.vector.reciprocal(r_inv[:], r_sum[:])
+        scatter(3 * PIECE, weights(3, "neg_last"))
+        factors = tile("factors", [P, 2], F32)
+        nc.scalar.activation(out=factors[:], in_=shares[:], func=ACT.Copy, scale=r_inv[:])
 
         for g, lo in enumerate(range(0, V, OUT_COLS)):
             hi = lo + OUT_COLS
-            mixed = sb.tile([P, hi - lo], F32, name="mixed%d" % g)
+            group = lo // EARLY
+            mixed = tile("mixed%d" % g, [P, OUT_COLS], F32)
             nc.vector.scalar_tensor_tensor(
-                out=mixed[:], in0=r_share[:, lo:hi], scalar=r_inv[:], in1=wf[:, lo:hi], op0=ALU.mult, op1=ALU.add
+                out=mixed[:],
+                in0=r_sb[:, lo:hi],
+                scalar=factors[:, group : group + 1],
+                in1=wf[:, lo:hi],
+                op0=ALU.mult,
+                op1=ALU.add,
             )
             queue = nc.scalar if g % 2 else nc.sync
             queue.dma_start(out=out[:, lo:hi], in_=mixed[:])

@@ -1,6 +1,7 @@
 from contextlib import ExitStack
 
 import concourse.mybir as mybir
+from concourse.masks import make_identity
 
 D, K, T, I, V, Q = 512, 512, 2048, 512, 1024, 128
 FLOPS = 2 * D * Q * I + 2 * K * Q * V
@@ -84,16 +85,11 @@ def tile_attend_knnlm_kernel(tc, query, keys_words, keys_scales, kn, hid, voc, l
         place_list = tile("place_list", [P, I // LANES], U16)
         lam_sb = tile("lam_sb", [P, 1], F32)
 
-        nc.gpsimd.memset(scale_pool[:].bitcast(I32), 0)
+        nc.vector.memset(scale_pool[:].bitcast(I32), 0)
+        nc.vector.memset(ident[:].bitcast(I32), 0)
         nc.vector.memset(kn_pool[0:KN_ROW, :].bitcast(I32), 0)
-        zeros = tile("zeros", [P, P], F32, tag="wf")
-        nc.gpsimd.memset(zeros[:], 0.0)
-        nc.gpsimd.affine_select(
-            out=ident[:], in_=zeros[:], compare_op=ALU.not_equal, fill=1.0, base=0, pattern=[[-1, P]], channel_multiplier=1
-        )
-        wf = tile("wf", [P, V], F32)
-        nc.gpsimd.memset(wf[:].bitcast(I32), 0)
         nc.gpsimd.dma_start(out=lam_sb[:], in_=lam)
+        make_identity(nc, ident[:], nomemset=True)
 
         nc.sync.dma_start(key_list[:], offs)
         nc.sync.dma_start(out=kn_pool[KN_ROW:P, :], in_=kn[0:1, :])
@@ -142,6 +138,8 @@ def tile_attend_knnlm_kernel(tc, query, keys_words, keys_scales, kn, hid, voc, l
                 nc.tensor.transpose(s_ps[:, lo + u * P : lo + (u + 1) * P], s_turned[:, u, :], ident[:])
 
         hid_codes, hid_scales = quantize("hid", cast("hid", hid_raw))
+        wf = tile("wf", [P, V], F32, tag="hid_bf")
+        nc.vector.memset(wf[:].bitcast(I32), 0)
         neg_early = tile("neg_early", [P, EARLY], F32)
         neg_last = tile("neg_last", [P, CHUNK], F32)
         grouped = {c: tile("voc%d_bf" % c, [P, CHUNK, PACK], BF16) for c in (0, 1, 3)}

@@ -26,6 +26,8 @@ N_CHUNKS = V // CHUNK
 EARLY = V - CHUNK
 HALF = I // 2
 PIECE = 128
+SHARE = 128
+SMALLEST_SHARE = 2.0**-64
 OUT_COLS = 256
 
 
@@ -83,13 +85,19 @@ def tile_attend_knnlm_kernel(tc, query, keys_words, keys_scales, kn, hid, voc, l
         ident = tile("ident", [P, P], F32)
         key_list = tile("key_list", [P, I // LANES], U16)
         place_list = tile("place_list", [P, I // LANES], U16)
-        lam_sb = tile("lam_sb", [P, 1], F32)
 
-        nc.vector.memset(scale_pool[:].bitcast(I32), 0)
-        nc.vector.memset(ident[:].bitcast(I32), 0)
-        nc.vector.memset(kn_pool[0:KN_ROW, :].bitcast(I32), 0)
-        nc.gpsimd.dma_start(out=lam_sb[:], in_=lam)
-        make_identity(nc, ident[:], nomemset=True)
+        lam_sb = tile("lam_sb", [P, 1], F32)
+        wf = tile("wf", [P, V], F32)
+
+        def zero_in_odd_runs(words):
+            cut = words.shape[1] // 2 + 1
+            nc.vector.memset(words[:, 0:cut], 0)
+            nc.vector.memset(words[:, cut:], 0)
+
+        zero_in_odd_runs(scale_pool[:].bitcast(I32))
+        zero_in_odd_runs(wf[:].bitcast(I32))
+        make_identity(nc, ident[:])
+        nc.gpsimd.memset(kn_pool[0:KN_ROW, :].bitcast(I32), 0)
 
         nc.sync.dma_start(key_list[:], offs)
         nc.sync.dma_start(out=kn_pool[KN_ROW:P, :], in_=kn[0:1, :])
@@ -98,23 +106,41 @@ def tile_attend_knnlm_kernel(tc, query, keys_words, keys_scales, kn, hid, voc, l
             nc.sync.dma_start(
                 out=scale_pool[row:P:32, :].bitcast(I32), in_=keys_scales[0, row:16:4, :].bitcast(I32)
             )
+        voc_raw = []
         nc.sync.dma_start(out=word_pool[:], in_=keys_words[0].rearrange("p n t -> p (n t)").bitcast(I32))
         hid_raw = load_rows("hid", hid)
-        voc_raw = [load_rows("voc0", voc[:, 0:CHUNK])]
-        nc.sync.dma_start(place_list[:], offs2)
-        for c in range(1, N_CHUNKS):
+        for c in range(N_CHUNKS):
             voc_raw.append(load_rows("voc%d" % c, voc[:, c * CHUNK : (c + 1) * CHUNK]))
+            if c == 1:
+                nc.sync.dma_start(place_list[:], offs2)
+            if c == 2:
+                nc.sync.dma_start(out=lam_sb[:], in_=lam)
+
+        neg_last = tile("neg_last", [P, CHUNK], F32)
+        b_first = ps.tile([P, CHUNK], F32, name="b_first")
+        b_pair = ps.tile([P, 2 * CHUNK], F32, name="b_pair")
+        b_last = ps.tile([P, CHUNK], F32, name="b_last")
+        b_ps = [b_first[:], b_pair[:, 0:CHUNK], b_pair[:, CHUNK:], b_last[:]]
+
+        def multiply(c, grouped):
+            codes, scales = quantize("voc%d" % c, grouped)
+            product(b_ps[c], (hid_codes[:], hid_scales[:]), (codes[:], scales[:]))
+
+        def lowest(name, dst, scores, start, tag):
+            low = tile(name, [P, 1], F32, tag=tag)
+            nc.vector.tensor_scalar(dst, scores, -1.0, start, ALU.mult, ALU.min, accum_out=low[:])
+            return low
 
         kn_listed = tile("kn_listed", [P, I], F32)
         nc.vector.tensor_copy(kn_listed[:], kn_pool[:].indirect(key_list[:]))
-        key_scales = tile("key_scales", [P, I], U8)
-        nc.vector.tensor_copy(key_scales[:], scale_pool[:].indirect(key_list[:]))
-        query_codes, query_scales = quantize("query", cast("query", query_raw))
         kn_turned = ps.tile([P, I // P, P], F32, name="kn_turned")
         for j in range(I // P):
             nc.tensor.transpose(kn_turned[:, j, :], kn_listed[:, j * P : (j + 1) * P], ident[:])
         neg_kn = tile("neg_kn", [P, I // P], F32)
         nc.scalar.activation(out=neg_kn[:], in_=kn_turned[:, :, KN_ROW], func=ACT.Copy, scale=-1.0)
+        key_scales = tile("key_scales", [P, I], U8)
+        nc.vector.tensor_copy(key_scales[:], scale_pool[:].indirect(key_list[:]))
+        query_codes, query_scales = quantize("query", cast("query", query_raw))
 
         s_ps = ps.tile([P, I], F32, name="s_ps")
         for h in range(2):
@@ -138,79 +164,59 @@ def tile_attend_knnlm_kernel(tc, query, keys_words, keys_scales, kn, hid, voc, l
                 nc.tensor.transpose(s_ps[:, lo + u * P : lo + (u + 1) * P], s_turned[:, u, :], ident[:])
 
         hid_codes, hid_scales = quantize("hid", cast("hid", hid_raw))
-        wf = tile("wf", [P, V], F32, tag="hid_bf")
-        nc.vector.memset(wf[:].bitcast(I32), 0)
         neg_early = tile("neg_early", [P, EARLY], F32)
-        neg_last = tile("neg_last", [P, CHUNK], F32)
-        grouped = {c: tile("voc%d_bf" % c, [P, CHUNK, PACK], BF16) for c in (0, 1, 3)}
-        b_ps = [ps.tile([P, CHUNK], F32, name="b_ps%d" % c) for c in range(N_CHUNKS)]
-        lows = []
-
-        def cast_cols(c, lo, hi, copy):
-            interleave(copy, grouped[c][:, lo:hi, :], voc_raw[c][:, :, lo:hi])
-
-        def multiply(c):
-            codes, scales = quantize("voc%d" % c, grouped[c])
-            product(b_ps[c][:], (hid_codes[:], hid_scales[:]), (codes[:], scales[:]))
-
-        def lowest(c):
-            dst = neg_last[:] if c == N_CHUNKS - 1 else neg_early[:, c * CHUNK : (c + 1) * CHUNK]
-            low = tile("low%d" % c, [P, 1], F32)
-            start = lows[-1][:] if lows else None
-            nc.vector.tensor_scalar(dst, b_ps[c][:], -1.0, start, ALU.mult, ALU.min, accum_out=low[:])
-            lows.append(low)
-
-        def scatter(lo, w):
-            hi = lo + w.shape[1]
-            nc.vector.tensor_copy(wf[:].indirect(place_list[:, lo // LANES : hi // LANES]), w[:])
-
-        def weights(n, tag):
-            w = tile("w%d" % n, [P, PIECE], F32, tag=tag)
-            nc.scalar.activation(out=w[:], in_=p_sb[:, n * PIECE : (n + 1) * PIECE], func=ACT.Copy, scale=w_factor[:])
-            return w
+        voc0_bf = tile("voc0_bf", [P, CHUNK, PACK], BF16)
+        interleave(nc.vector.tensor_copy, voc0_bf[:], voc_raw[0][:])
+        multiply(0, voc0_bf)
+        neg_max = tile("neg_max", [P, 1], F32, tag="voc0_raw")
+        nc.vector.tensor_reduce(out=neg_max[:], in_=s_ps[:], axis=AX.X, op=ALU.max, negate=True)
+        low_first = lowest("low_first", neg_early[:, 0:CHUNK], b_first[:], None, None)
 
         knn_share = tile("knn_share", [P, 1], F32)
         shares = tile("shares", [P, 2], F32)
-        nc.gpsimd.tensor_scalar(knn_share[:], lam_sb[:], 512.0, 0.0, ALU.mult, ALU.add)
+        nc.gpsimd.tensor_scalar(knn_share[:], lam_sb[:], 512.0, SMALLEST_SHARE, ALU.mult, ALU.max)
         nc.gpsimd.tensor_scalar(shares[:, 1:2], lam_sb[:], -512.0, 512.0, ALU.mult, ALU.add)
+        share_inv = tile("share_inv", [P, 1], F32)
+        nc.vector.reciprocal(share_inv[:], knn_share[:])
 
-        cast_cols(0, 0, CHUNK, nc.vector.tensor_copy)
-        multiply(0)
-        neg_max = tile("neg_max", [P, 1], F32, tag="voc0_raw")
-        nc.vector.tensor_reduce(out=neg_max[:], in_=s_ps[:], axis=AX.X, op=ALU.max, negate=True)
-        lowest(0)
-        cast_cols(1, 0, CHUNK, act_copy)
-        p_sb = tile("p_sb", [P, I], F32, tag="voc1_raw")
-        p_sum = tile("p_sum", [P, 1], F32)
-        nc.scalar.activation(out=p_sb[:], in_=s_ps[:], func=ACT.Exp, bias=neg_max[:], accum_out=p_sum[:])
-        multiply(1)
-        grouped.setdefault(2, tile("voc2_bf", [P, CHUNK, PACK], BF16, tag="voc0_raw"))
-        cast_cols(2, 0, CHUNK // 2, nc.vector.tensor_copy)
-        cast_cols(2, CHUNK // 2, CHUNK, act_copy)
-        p_inv = tile("p_inv", [P, 1], F32)
-        nc.vector.reciprocal(p_inv[:], p_sum[:])
-        lowest(1)
-        w_first = tile("w_first", [P, PIECE], F32)
-        nc.vector.tensor_scalar(w_first[:], p_sb[:, 0:PIECE], p_inv[:], knn_share[:], ALU.mult, ALU.mult)
-        w_factor = tile("w_factor", [P, 1], F32)
-        nc.vector.tensor_scalar(w_factor[:], p_inv[:], knn_share[:], None, ALU.mult)
-        multiply(2)
-        scatter(0, w_first)
-        lowest(2)
-        cast_cols(3, 0, CHUNK, act_copy)
-        multiply(3)
-        scatter(PIECE, weights(1, "voc3_raw"))
+        p_sums = tile("p_sums", [P, I // PIECE], F32)
+
+        def weights(n, tag):
+            p = tile("p%d" % n, [P, PIECE], F32, tag=tag)
+            nc.scalar.activation(
+                out=p[:],
+                in_=s_ps[:, n * PIECE : (n + 1) * PIECE],
+                func=ACT.Exp,
+                bias=neg_max[:],
+                accum_out=p_sums[:, n : n + 1],
+            )
+            return p
+
+        def scatter(n, p):
+            offsets = place_list[:, n * PIECE // LANES : (n + 1) * PIECE // LANES]
+            nc.vector.tensor_copy(wf[:].indirect(offsets), p[:])
+
+        voc1_bf = cast("voc1", voc_raw[1])
+        p_first = weights(0, "voc1_raw")
+        multiply(1, voc1_bf)
+        scatter(0, p_first)
+        multiply(2, cast("voc2", voc_raw[2]))
+        voc3_bf = tile("voc3_bf", [P, CHUNK, PACK], BF16)
+        interleave(nc.vector.tensor_copy, voc3_bf[:, 0:SHARE, :], voc_raw[3][:, :, 0:SHARE])
+        interleave(act_copy, voc3_bf[:, SHARE:, :], voc_raw[3][:, :, SHARE:])
+        multiply(3, voc3_bf)
+        low_early = lowest("low_early", neg_early[:, CHUNK:EARLY], b_pair[:], low_first[:], "voc3_raw")
+        scatter(1, weights(1, "voc3_bf"))
+        p_third = weights(2, "low_first")
 
         r_sb = tile("r_sb", [P, V], F32)
         sum_early = tile("sum_early", [P, 1], F32)
         sum_last = tile("sum_last", [P, 1], F32)
-        low_early = lows[-1]
         nc.scalar.activation(
             out=r_sb[:, 0:EARLY], in_=neg_early[:], func=ACT.Exp, scale=-1.0, bias=low_early[:], accum_out=sum_early[:]
         )
-        lowest(3)
-        low_last = lows[-1]
-        scatter(2 * PIECE, weights(2, "voc3_codes"))
+        low_last = lowest("low_last", neg_last[:], b_last[:], low_early[:], None)
+        scatter(2, p_third)
         shrink = tile("shrink", [P, 1], F32)
         nc.scalar.activation(out=shrink[:], in_=low_early[:], func=ACT.Exp, scale=-1.0, bias=low_last[:])
         nc.scalar.activation(
@@ -221,21 +227,24 @@ def tile_attend_knnlm_kernel(tc, query, keys_words, keys_scales, kn, hid, voc, l
         nc.scalar.activation(out=r_sum[:], in_=sum_early[:], func=ACT.Identity, scale=shrink[:], bias=sum_last[:])
         r_inv = tile("r_inv", [P, 1], F32)
         nc.vector.reciprocal(r_inv[:], r_sum[:])
-        scatter(3 * PIECE, weights(3, "neg_last"))
+        scatter(3, weights(3, "neg_last"))
         factors = tile("factors", [P, 2], F32)
         nc.scalar.activation(out=factors[:], in_=shares[:], func=ACT.Copy, scale=r_inv[:])
+        parts_over_share = tile("parts_over_share", [P, I // PIECE], F32)
+        p_over_share = tile("p_over_share", [P, 1], F32)
+        nc.scalar.activation(
+            out=parts_over_share[:], in_=p_sums[:], func=ACT.Copy, scale=share_inv[:], accum_out=p_over_share[:]
+        )
+        knn_factor = tile("knn_factor", [P, 1], F32)
+        nc.vector.reciprocal(knn_factor[:], p_over_share[:])
 
         for g, lo in enumerate(range(0, V, OUT_COLS)):
             hi = lo + OUT_COLS
             group = lo // EARLY
+            lm = tile("lm%d" % g, [P, OUT_COLS], F32)
+            nc.scalar.activation(out=lm[:], in_=r_sb[:, lo:hi], func=ACT.Copy, scale=factors[:, group : group + 1])
             mixed = tile("mixed%d" % g, [P, OUT_COLS], F32)
             nc.vector.scalar_tensor_tensor(
-                out=mixed[:],
-                in0=r_sb[:, lo:hi],
-                scalar=factors[:, group : group + 1],
-                in1=wf[:, lo:hi],
-                op0=ALU.mult,
-                op1=ALU.add,
+                out=mixed[:], in0=wf[:, lo:hi], scalar=knn_factor[:], in1=lm[:], op0=ALU.mult, op1=ALU.add
             )
-            queue = nc.scalar if g % 2 else nc.sync
-            queue.dma_start(out=out[:, lo:hi], in_=mixed[:])
+            nc.sync.dma_start(out=out[:, lo:hi], in_=mixed[:])

@@ -28,7 +28,7 @@ HALF = I // 2
 PIECE = 128
 SHARE = 128
 SMALLEST_SHARE = 2.0**-64
-OUT_COLS = 256
+OUT_PIECES = ((0, 256), (256, 512), (512, 768), (768, 1024))
 
 
 def tile_attend_knnlm_kernel(tc, query, keys_words, keys_scales, kn, hid, voc, lam, offs, offs2, out):
@@ -86,7 +86,6 @@ def tile_attend_knnlm_kernel(tc, query, keys_words, keys_scales, kn, hid, voc, l
         key_list = tile("key_list", [P, I // LANES], U16)
         place_list = tile("place_list", [P, I // LANES], U16)
 
-        lam_sb = tile("lam_sb", [P, 1], F32)
         wf = tile("wf", [P, V], F32)
 
         def zero_in_odd_runs(words):
@@ -113,8 +112,8 @@ def tile_attend_knnlm_kernel(tc, query, keys_words, keys_scales, kn, hid, voc, l
             voc_raw.append(load_rows("voc%d" % c, voc[:, c * CHUNK : (c + 1) * CHUNK]))
             if c == 1:
                 nc.sync.dma_start(place_list[:], offs2)
-            if c == 2:
-                nc.sync.dma_start(out=lam_sb[:], in_=lam)
+        lam_sb = tile("lam_sb", [P, 1], F32)
+        nc.sync.dma_start(out=lam_sb[:], in_=lam)
 
         neg_last = tile("neg_last", [P, CHUNK], F32)
         b_first = ps.tile([P, CHUNK], F32, name="b_first")
@@ -172,13 +171,6 @@ def tile_attend_knnlm_kernel(tc, query, keys_words, keys_scales, kn, hid, voc, l
         nc.vector.tensor_reduce(out=neg_max[:], in_=s_ps[:], axis=AX.X, op=ALU.max, negate=True)
         low_first = lowest("low_first", neg_early[:, 0:CHUNK], b_first[:], None, None)
 
-        knn_share = tile("knn_share", [P, 1], F32)
-        shares = tile("shares", [P, 2], F32)
-        nc.gpsimd.tensor_scalar(knn_share[:], lam_sb[:], 512.0, SMALLEST_SHARE, ALU.mult, ALU.max)
-        nc.gpsimd.tensor_scalar(shares[:, 1:2], lam_sb[:], -512.0, 512.0, ALU.mult, ALU.add)
-        share_inv = tile("share_inv", [P, 1], F32)
-        nc.vector.reciprocal(share_inv[:], knn_share[:])
-
         p_sums = tile("p_sums", [P, I // PIECE], F32)
 
         def weights(n, tag):
@@ -209,6 +201,13 @@ def tile_attend_knnlm_kernel(tc, query, keys_words, keys_scales, kn, hid, voc, l
         scatter(1, weights(1, "voc3_bf"))
         p_third = weights(2, "low_first")
 
+        knn_share = tile("knn_share", [P, 1], F32, tag="voc3_codes")
+        shares = tile("shares", [P, 2], F32, tag="voc3_scales")
+        nc.scalar.activation(out=knn_share[:], in_=lam_sb[:], func=ACT.Copy, scale=512.0, bias=SMALLEST_SHARE)
+        nc.scalar.activation(out=shares[:, 1:2], in_=lam_sb[:], func=ACT.Copy, scale=-512.0, bias=512.0)
+        share_inv = tile("share_inv", [P, 1], F32, tag="voc3_bf")
+        nc.vector.reciprocal(share_inv[:], knn_share[:])
+
         r_sb = tile("r_sb", [P, V], F32)
         sum_early = tile("sum_early", [P, 1], F32)
         sum_last = tile("sum_last", [P, 1], F32)
@@ -238,12 +237,11 @@ def tile_attend_knnlm_kernel(tc, query, keys_words, keys_scales, kn, hid, voc, l
         knn_factor = tile("knn_factor", [P, 1], F32)
         nc.vector.reciprocal(knn_factor[:], p_over_share[:])
 
-        for g, lo in enumerate(range(0, V, OUT_COLS)):
-            hi = lo + OUT_COLS
+        for g, (lo, hi) in enumerate(OUT_PIECES):
             group = lo // EARLY
-            lm = tile("lm%d" % g, [P, OUT_COLS], F32)
+            lm = tile("lm%d" % g, [P, hi - lo], F32)
             nc.scalar.activation(out=lm[:], in_=r_sb[:, lo:hi], func=ACT.Copy, scale=factors[:, group : group + 1])
-            mixed = tile("mixed%d" % g, [P, OUT_COLS], F32)
+            mixed = tile("mixed%d" % g, [P, hi - lo], F32)
             nc.vector.scalar_tensor_tensor(
                 out=mixed[:], in0=wf[:, lo:hi], scalar=knn_factor[:], in1=lm[:], op0=ALU.mult, op1=ALU.add
             )

@@ -21,6 +21,7 @@ P = 128
 PACK = 4
 LANES = 16
 KN_ROW = P - 1
+KN_VECTOR = 896
 CHUNK = 256
 N_CHUNKS = V // CHUNK
 EARLY = V - CHUNK
@@ -86,17 +87,18 @@ def tile_attend_knnlm_kernel(tc, query, keys_words, keys_scales, kn, hid, voc, l
         key_list = tile("key_list", [P, I // LANES], U16)
         place_list = tile("place_list", [P, I // LANES], U16)
 
-        wf = tile("wf", [P, V], F32)
-
         def zero_in_odd_runs(words):
             cut = words.shape[1] // 2 + 1
             nc.vector.memset(words[:, 0:cut], 0)
             nc.vector.memset(words[:, cut:], 0)
 
         zero_in_odd_runs(scale_pool[:].bitcast(I32))
-        zero_in_odd_runs(wf[:].bitcast(I32))
+        kn_words = kn_pool[0:KN_ROW, :].bitcast(I32)
+        zero_in_odd_runs(kn_words[:, 0:KN_VECTOR])
+        wf = tile("wf", [P, V], F32)
+        nc.vector.memset(wf[:].bitcast(I32), 0)
         make_identity(nc, ident[:])
-        nc.gpsimd.memset(kn_pool[0:KN_ROW, :].bitcast(I32), 0)
+        nc.gpsimd.memset(kn_words[:, KN_VECTOR:], 0)
 
         nc.sync.dma_start(key_list[:], offs)
         nc.sync.dma_start(out=kn_pool[KN_ROW:P, :], in_=kn[0:1, :])

@@ -21,15 +21,14 @@ P = 128
 PACK = 4
 LANES = 16
 KN_ROW = P - 1
+CHUNKS = ((0, 256), (256, 512), (512, 768), (768, 1024))
+FIRST = 256
+EARLY = 768
+PIECE = 256
+TAIL = 128
 KN_VECTOR = 896
-CHUNK = 256
-N_CHUNKS = V // CHUNK
-EARLY = V - CHUNK
 HALF = I // 2
-PIECE = 128
-SHARE = 128
 SMALLEST_SHARE = 2.0**-64
-OUT_PIECES = ((0, 256), (256, 512), (512, 768), (768, 1024))
 
 
 def tile_attend_knnlm_kernel(tc, query, keys_words, keys_scales, kn, hid, voc, lam, offs, offs2, out):
@@ -55,9 +54,9 @@ def tile_attend_knnlm_kernel(tc, query, keys_words, keys_scales, kn, hid, voc, l
                 in_=raw.rearrange("p t (c i) -> p c t i", i=4),
             )
 
-        def cast(name, raw):
+        def cast(name, raw, copy):
             grouped = tile(name + "_bf", [P, raw.shape[2], PACK], BF16)
-            interleave(act_copy, grouped[:], raw[:])
+            interleave(copy, grouped[:], raw[:])
             return grouped
 
         def quantize(name, grouped):
@@ -86,6 +85,7 @@ def tile_attend_knnlm_kernel(tc, query, keys_words, keys_scales, kn, hid, voc, l
         ident = tile("ident", [P, P], F32)
         key_list = tile("key_list", [P, I // LANES], U16)
         place_list = tile("place_list", [P, I // LANES], U16)
+        wf = tile("wf", [P, V], F32)
 
         def zero_in_odd_runs(words):
             cut = words.shape[1] // 2 + 1
@@ -95,156 +95,155 @@ def tile_attend_knnlm_kernel(tc, query, keys_words, keys_scales, kn, hid, voc, l
         zero_in_odd_runs(scale_pool[:].bitcast(I32))
         kn_words = kn_pool[0:KN_ROW, :].bitcast(I32)
         zero_in_odd_runs(kn_words[:, 0:KN_VECTOR])
-        wf = tile("wf", [P, V], F32)
         nc.vector.memset(wf[:].bitcast(I32), 0)
         make_identity(nc, ident[:])
         nc.gpsimd.memset(kn_words[:, KN_VECTOR:], 0)
 
+        query_raw = load_rows("query", query)
         nc.sync.dma_start(key_list[:], offs)
         nc.sync.dma_start(out=kn_pool[KN_ROW:P, :], in_=kn[0:1, :])
-        query_raw = load_rows("query", query)
         for row in range(4):
             nc.sync.dma_start(
                 out=scale_pool[row:P:32, :].bitcast(I32), in_=keys_scales[0, row:16:4, :].bitcast(I32)
             )
-        voc_raw = []
         nc.sync.dma_start(out=word_pool[:], in_=keys_words[0].rearrange("p n t -> p (n t)").bitcast(I32))
         hid_raw = load_rows("hid", hid)
-        for c in range(N_CHUNKS):
-            voc_raw.append(load_rows("voc%d" % c, voc[:, c * CHUNK : (c + 1) * CHUNK]))
+        voc_raw = []
+        lam_sb = tile("lam_sb", [P, 1], F32)
+        for c, (lo, hi) in enumerate(CHUNKS):
+            voc_raw.append(load_rows("voc%d" % c, voc[:, lo:hi]))
+            if c == 0:
+                nc.sync.dma_start(out=lam_sb[:], in_=lam)
             if c == 1:
                 nc.sync.dma_start(place_list[:], offs2)
-        lam_sb = tile("lam_sb", [P, 1], F32)
-        nc.sync.dma_start(out=lam_sb[:], in_=lam)
 
-        neg_last = tile("neg_last", [P, CHUNK], F32)
-        b_first = ps.tile([P, CHUNK], F32, name="b_first")
-        b_pair = ps.tile([P, 2 * CHUNK], F32, name="b_pair")
-        b_last = ps.tile([P, CHUNK], F32, name="b_last")
-        b_ps = [b_first[:], b_pair[:, 0:CHUNK], b_pair[:, CHUNK:], b_last[:]]
-
-        def multiply(c, grouped):
-            codes, scales = quantize("voc%d" % c, grouped)
-            product(b_ps[c], (hid_codes[:], hid_scales[:]), (codes[:], scales[:]))
-
-        def lowest(name, dst, scores, start, tag):
-            low = tile(name, [P, 1], F32, tag=tag)
-            nc.vector.tensor_scalar(dst, scores, -1.0, start, ALU.mult, ALU.min, accum_out=low[:])
-            return low
-
-        kn_listed = tile("kn_listed", [P, I], F32)
-        nc.vector.tensor_copy(kn_listed[:], kn_pool[:].indirect(key_list[:]))
-        kn_turned = ps.tile([P, I // P, P], F32, name="kn_turned")
-        for j in range(I // P):
-            nc.tensor.transpose(kn_turned[:, j, :], kn_listed[:, j * P : (j + 1) * P], ident[:])
+        query_bf = cast("query", query_raw, act_copy)
+        kn_listed = tile("kn_listed", [P, I], F32, tag="query_raw")
         neg_kn = tile("neg_kn", [P, I // P], F32)
-        nc.scalar.activation(out=neg_kn[:], in_=kn_turned[:, :, KN_ROW], func=ACT.Copy, scale=-1.0)
-        key_scales = tile("key_scales", [P, I], U8)
-        nc.vector.tensor_copy(key_scales[:], scale_pool[:].indirect(key_list[:]))
-        query_codes, query_scales = quantize("query", cast("query", query_raw))
-
-        s_ps = ps.tile([P, I], F32, name="s_ps")
+        blocks = HALF // P
         for h in range(2):
             lo = h * HALF
-            key_words = tile("key_words%d" % h, [P, HALF], I32)
+            act_copy(kn_listed[:, lo : lo + HALF], kn_pool[:].indirect(key_list[:, lo // LANES : (lo + HALF) // LANES]))
+        for h in range(2):
+            kn_turned = ps.tile([P, blocks, P], F32, name="kn_turned%d" % h, tag="a_bank%d" % (h * blocks))
+            for u in range(blocks):
+                lo = (h * blocks + u) * P
+                nc.tensor.transpose(kn_turned[:, u, :], kn_listed[:, lo : lo + P], ident[:])
+            nc.scalar.activation(
+                out=neg_kn[:, h * blocks : (h + 1) * blocks], in_=kn_turned[:, :, KN_ROW], func=ACT.Copy, scale=-1.0
+            )
+
+        key_scales = tile("key_scales", [P, I], U8)
+        nc.vector.tensor_copy(key_scales[:], scale_pool[:].indirect(key_list[:]))
+        query_codes, query_scales = quantize("query", query_bf)
+
+        hid_bf = cast("hid", hid_raw, act_copy)
+        s_turned = tile("s_turned", [P, I // P, Q], F32, tag="hid_raw")
+        s_ps = ps.tile([P, I], F32, name="s_ps")
+        for j in range(I // P):
+            lo = j * P
+            key_words = tile("key_words%d" % j, [P, P], I32)
             nc.vector.tensor_copy(
                 key_words[:].bitcast(U32),
-                word_pool[:].bitcast(U32).indirect(key_list[:, lo // LANES : (lo + HALF) // LANES]),
+                word_pool[:].bitcast(U32).indirect(key_list[:, lo // LANES : (lo + P) // LANES]),
             )
-            a_ps = ps.tile([P, HALF // P, Q], F32, name="a_ps%d" % h)
-            s_turned = tile("s_turned%d" % h, [P, HALF // P, Q], F32)
-            for u in range(HALF // P):
-                keys = (key_words[:, u * P : (u + 1) * P], key_scales[:, lo + u * P : lo + (u + 1) * P])
-                product(a_ps[:, u, :], keys, (query_codes[:], query_scales[:]))
-            for u in range(HALF // P):
-                j = lo // P + u
-                nc.scalar.activation(
-                    out=s_turned[:, u, :], in_=a_ps[:, u, :], func=ACT.Identity, scale=2.0, bias=neg_kn[:, j : j + 1]
-                )
-            for u in range(HALF // P):
-                nc.tensor.transpose(s_ps[:, lo + u * P : lo + (u + 1) * P], s_turned[:, u, :], ident[:])
+            a_ps = ps.tile([P, Q], F32, name="a_ps%d" % j, tag="a_bank%d" % j)
+            product(a_ps[:], (key_words[:], key_scales[:, lo : lo + P]), (query_codes[:], query_scales[:]))
+            nc.scalar.activation(
+                out=s_turned[:, j, :], in_=a_ps[:], func=ACT.Identity, scale=2.0, bias=neg_kn[:, j : j + 1]
+            )
+            nc.tensor.transpose(s_ps[:, lo : lo + P], s_turned[:, j, :], ident[:])
 
-        hid_codes, hid_scales = quantize("hid", cast("hid", hid_raw))
-        neg_early = tile("neg_early", [P, EARLY], F32)
-        voc0_bf = tile("voc0_bf", [P, CHUNK, PACK], BF16)
-        interleave(nc.vector.tensor_copy, voc0_bf[:], voc_raw[0][:])
-        multiply(0, voc0_bf)
+        hid_codes, hid_scales = quantize("hid", hid_bf)
+
+        neg_b = tile("neg_b", [P, V], F32)
+
+        def multiply(name, grouped):
+            codes, scales = quantize(name, grouped)
+            b_ps = ps.tile([P, grouped.shape[1]], F32, name=name + "_ps")
+            product(b_ps[:], (hid_codes[:], hid_scales[:]), (codes[:], scales[:]))
+            return b_ps
+
+        def lowest(low, lo, b_ps, start):
+            nc.vector.tensor_scalar(
+                neg_b[:, lo : lo + b_ps.shape[1]], b_ps[:], -1.0, start, ALU.mult, ALU.min, accum_out=low
+            )
+            return low
+
+        b_first = multiply("first", cast("voc0", voc_raw[0], nc.vector.tensor_copy))
+        middle_bf = tile("middle_bf", [P, EARLY - FIRST, PACK], BF16)
+        cut = voc_raw[1].shape[2]
+        interleave(act_copy, middle_bf[:, 0:cut, :], voc_raw[1][:])
         neg_max = tile("neg_max", [P, 1], F32, tag="voc0_raw")
         nc.vector.tensor_reduce(out=neg_max[:], in_=s_ps[:], axis=AX.X, op=ALU.max, negate=True)
-        low_first = lowest("low_first", neg_early[:, 0:CHUNK], b_first[:], None, None)
 
-        p_sums = tile("p_sums", [P, I // PIECE], F32)
+        knn_share = tile("knn_share", [P, 1], F32)
+        lm_share = tile("lm_share", [P, 1], F32)
+        lm_divisor = tile("lm_divisor", [P, 1], F32)
+        nc.scalar.activation(out=knn_share[:], in_=lam_sb[:], func=ACT.Copy, scale=512.0)
+        nc.scalar.activation(out=lm_share[:], in_=lam_sb[:], func=ACT.Copy, scale=-512.0, bias=512.0)
+        nc.scalar.activation(out=lm_divisor[:], in_=lm_share[:], func=ACT.Copy, bias=SMALLEST_SHARE)
 
-        def weights(n, tag):
-            p = tile("p%d" % n, [P, PIECE], F32, tag=tag)
-            nc.scalar.activation(
-                out=p[:],
-                in_=s_ps[:, n * PIECE : (n + 1) * PIECE],
-                func=ACT.Exp,
-                bias=neg_max[:],
-                accum_out=p_sums[:, n : n + 1],
-            )
-            return p
+        share_inv = tile("share_inv", [P, 1], F32)
+        nc.vector.reciprocal(share_inv[:], lm_divisor[:])
 
-        def scatter(n, p):
-            offsets = place_list[:, n * PIECE // LANES : (n + 1) * PIECE // LANES]
-            nc.vector.tensor_copy(wf[:].indirect(offsets), p[:])
+        def weights(name, lo, hi, tag=None):
+            p = tile(name, [P, hi - lo], F32, tag=tag)
+            p_sum = tile(name + "_sum", [P, 1], F32)
+            nc.scalar.activation(out=p[:], in_=s_ps[:, lo:hi], func=ACT.Exp, bias=neg_max[:], accum_out=p_sum[:])
+            return p, p_sum
 
-        voc1_bf = cast("voc1", voc_raw[1])
-        p_first = weights(0, "voc1_raw")
-        multiply(1, voc1_bf)
-        scatter(0, p_first)
-        multiply(2, cast("voc2", voc_raw[2]))
-        voc3_bf = tile("voc3_bf", [P, CHUNK, PACK], BF16)
-        interleave(nc.vector.tensor_copy, voc3_bf[:, 0:SHARE, :], voc_raw[3][:, :, 0:SHARE])
-        interleave(act_copy, voc3_bf[:, SHARE:, :], voc_raw[3][:, :, SHARE:])
-        multiply(3, voc3_bf)
-        low_early = lowest("low_early", neg_early[:, CHUNK:EARLY], b_pair[:], low_first[:], "voc3_raw")
-        scatter(1, weights(1, "voc3_bf"))
-        p_third = weights(2, "low_first")
+        def places(lo, hi):
+            return wf[:].indirect(place_list[:, lo // LANES : hi // LANES])
 
-        knn_share = tile("knn_share", [P, 1], F32, tag="voc3_codes")
-        shares = tile("shares", [P, 2], F32, tag="voc3_scales")
-        nc.scalar.activation(out=knn_share[:], in_=lam_sb[:], func=ACT.Copy, scale=512.0, bias=SMALLEST_SHARE)
-        nc.scalar.activation(out=shares[:, 1:2], in_=lam_sb[:], func=ACT.Copy, scale=-512.0, bias=512.0)
-        share_inv = tile("share_inv", [P, 1], F32, tag="voc3_bf")
-        nc.vector.reciprocal(share_inv[:], knn_share[:])
+        p_head, p_head_sum = weights("p_head", 0, I - TAIL, tag="voc1_raw")
+        act_copy(places(0, I - TAIL), p_head[:])
+
+        low_first = lowest(tile("low_first", [P, 1], F32)[:], 0, b_first, None)
+        interleave(nc.vector.tensor_copy, middle_bf[:, cut:, :], voc_raw[2][:])
+        b_middle = multiply("middle", middle_bf)
+        last_bf = cast("voc3", voc_raw[3], nc.vector.tensor_copy)
+        low_early = lowest(tile("low_early", [P, 1], F32)[:], FIRST, b_middle, low_first)
+        b_last = multiply("last", last_bf)
+        p_tail, p_tail_sum = weights("p_tail", I - TAIL, I, tag="voc3_raw")
+        p_total = tile("p_total", [P, 1], F32)
+        nc.scalar.activation(out=p_total[:], in_=p_head_sum[:], func=ACT.Identity, bias=p_tail_sum[:])
+        nc.vector.tensor_copy(places(I - TAIL, I), p_tail[:])
+        p_inv = tile("p_inv", [P, 1], F32)
+        nc.vector.reciprocal(p_inv[:], p_total[:])
 
         r_sb = tile("r_sb", [P, V], F32)
         sum_early = tile("sum_early", [P, 1], F32)
         sum_last = tile("sum_last", [P, 1], F32)
         nc.scalar.activation(
-            out=r_sb[:, 0:EARLY], in_=neg_early[:], func=ACT.Exp, scale=-1.0, bias=low_early[:], accum_out=sum_early[:]
+            out=r_sb[:, 0:EARLY], in_=neg_b[:, 0:EARLY], func=ACT.Exp, scale=-1.0, bias=low_early, accum_out=sum_early[:]
         )
-        low_last = lowest("low_last", neg_last[:], b_last[:], low_early[:], None)
-        scatter(2, p_third)
+        early_over_share = tile("early_over_share", [P, 1], F32)
+        nc.scalar.activation(out=early_over_share[:], in_=sum_early[:], func=ACT.Copy, scale=share_inv[:])
+        low_last = lowest(tile("low_last", [P, 1], F32)[:], EARLY, b_last, low_early)
+        knn_part = tile("knn_part", [P, V], F32, tag="last_codes")
+        nc.vector.tensor_scalar(knn_part[:], wf[:], p_inv[:], knn_share[:], ALU.mult, ALU.mult)
         shrink = tile("shrink", [P, 1], F32)
-        nc.scalar.activation(out=shrink[:], in_=low_early[:], func=ACT.Exp, scale=-1.0, bias=low_last[:])
+        nc.scalar.activation(out=shrink[:], in_=low_early, func=ACT.Exp, scale=-1.0, bias=low_last)
         nc.scalar.activation(
-            out=r_sb[:, EARLY:V], in_=neg_last[:], func=ACT.Exp, scale=-1.0, bias=low_last[:], accum_out=sum_last[:]
+            out=r_sb[:, EARLY:V], in_=neg_b[:, EARLY:V], func=ACT.Exp, scale=-1.0, bias=low_last, accum_out=sum_last[:]
         )
-        nc.scalar.activation(out=shares[:, 0:1], in_=shares[:, 1:2], func=ACT.Copy, scale=shrink[:])
-        r_sum = tile("r_sum", [P, 1], F32)
-        nc.scalar.activation(out=r_sum[:], in_=sum_early[:], func=ACT.Identity, scale=shrink[:], bias=sum_last[:])
-        r_inv = tile("r_inv", [P, 1], F32)
-        nc.vector.reciprocal(r_inv[:], r_sum[:])
-        scatter(3, weights(3, "neg_last"))
-        factors = tile("factors", [P, 2], F32)
-        nc.scalar.activation(out=factors[:], in_=shares[:], func=ACT.Copy, scale=r_inv[:])
-        parts_over_share = tile("parts_over_share", [P, I // PIECE], F32)
-        p_over_share = tile("p_over_share", [P, 1], F32)
+        early_term = tile("early_term", [P, 1], F32)
+        nc.scalar.activation(out=early_term[:], in_=early_over_share[:], func=ACT.Copy, scale=shrink[:])
+        sum_over_share = tile("sum_over_share", [P, 1], F32)
         nc.scalar.activation(
-            out=parts_over_share[:], in_=p_sums[:], func=ACT.Copy, scale=share_inv[:], accum_out=p_over_share[:]
+            out=sum_over_share[:], in_=sum_last[:], func=ACT.Identity, scale=share_inv[:], bias=early_term[:]
         )
-        knn_factor = tile("knn_factor", [P, 1], F32)
-        nc.vector.reciprocal(knn_factor[:], p_over_share[:])
+        factor_last = tile("factor_last", [P, 1], F32)
+        nc.vector.reciprocal(factor_last[:], sum_over_share[:])
+        factor_early = tile("factor_early", [P, 1], F32)
+        nc.scalar.activation(out=factor_early[:], in_=factor_last[:], func=ACT.Copy, scale=shrink[:])
 
-        for g, (lo, hi) in enumerate(OUT_PIECES):
-            group = lo // EARLY
-            lm = tile("lm%d" % g, [P, hi - lo], F32)
-            nc.scalar.activation(out=lm[:], in_=r_sb[:, lo:hi], func=ACT.Copy, scale=factors[:, group : group + 1])
-            mixed = tile("mixed%d" % g, [P, hi - lo], F32)
+        for c in (3, 0, 1, 2):
+            lo, hi = c * PIECE, (c + 1) * PIECE
+            factor = factor_last if lo >= EARLY else factor_early
+            mixed = tile("mixed%d" % c, [P, PIECE], F32)
             nc.vector.scalar_tensor_tensor(
-                out=mixed[:], in0=wf[:, lo:hi], scalar=knn_factor[:], in1=lm[:], op0=ALU.mult, op1=ALU.add
+                out=mixed[:], in0=r_sb[:, lo:hi], scalar=factor[:], in1=knn_part[:, lo:hi], op0=ALU.mult, op1=ALU.add
             )
             nc.sync.dma_start(out=out[:, lo:hi], in_=mixed[:])

@@ -26,7 +26,6 @@ FIRST = 256
 EARLY = 768
 PIECE = 256
 TAIL = 128
-KN_VECTOR = 896
 HALF = I // 2
 SMALLEST_SHARE = 2.0**-64
 
@@ -87,17 +86,11 @@ def tile_attend_knnlm_kernel(tc, query, keys_words, keys_scales, kn, hid, voc, l
         place_list = tile("place_list", [P, I // LANES], U16)
         wf = tile("wf", [P, V], F32)
 
-        def zero_in_odd_runs(words):
-            cut = words.shape[1] // 2 + 1
-            nc.vector.memset(words[:, 0:cut], 0)
-            nc.vector.memset(words[:, cut:], 0)
-
-        zero_in_odd_runs(scale_pool[:].bitcast(I32))
-        kn_words = kn_pool[0:KN_ROW, :].bitcast(I32)
-        zero_in_odd_runs(kn_words[:, 0:KN_VECTOR])
+        nc.vector.memset(scale_pool[:].bitcast(I32), 0)
+        nc.vector.memset(ident[:], 0.0)
+        make_identity(nc, ident[:], nomemset=True)
+        nc.vector.memset(kn_pool[0:KN_ROW, :].bitcast(I32), 0)
         nc.vector.memset(wf[:].bitcast(I32), 0)
-        make_identity(nc, ident[:])
-        nc.gpsimd.memset(kn_words[:, KN_VECTOR:], 0)
 
         query_raw = load_rows("query", query)
         nc.sync.dma_start(key_list[:], offs)
@@ -112,10 +105,9 @@ def tile_attend_knnlm_kernel(tc, query, keys_words, keys_scales, kn, hid, voc, l
         lam_sb = tile("lam_sb", [P, 1], F32)
         for c, (lo, hi) in enumerate(CHUNKS):
             voc_raw.append(load_rows("voc%d" % c, voc[:, lo:hi]))
-            if c == 0:
-                nc.sync.dma_start(out=lam_sb[:], in_=lam)
-            if c == 1:
+            if c == 2:
                 nc.sync.dma_start(place_list[:], offs2)
+        nc.sync.dma_start(out=lam_sb[:], in_=lam)
 
         query_bf = cast("query", query_raw, act_copy)
         kn_listed = tile("kn_listed", [P, I], F32, tag="query_raw")
@@ -177,16 +169,6 @@ def tile_attend_knnlm_kernel(tc, query, keys_words, keys_scales, kn, hid, voc, l
         neg_max = tile("neg_max", [P, 1], F32, tag="voc0_raw")
         nc.vector.tensor_reduce(out=neg_max[:], in_=s_ps[:], axis=AX.X, op=ALU.max, negate=True)
 
-        knn_share = tile("knn_share", [P, 1], F32)
-        lm_share = tile("lm_share", [P, 1], F32)
-        lm_divisor = tile("lm_divisor", [P, 1], F32)
-        nc.scalar.activation(out=knn_share[:], in_=lam_sb[:], func=ACT.Copy, scale=512.0)
-        nc.scalar.activation(out=lm_share[:], in_=lam_sb[:], func=ACT.Copy, scale=-512.0, bias=512.0)
-        nc.scalar.activation(out=lm_divisor[:], in_=lm_share[:], func=ACT.Copy, bias=SMALLEST_SHARE)
-
-        share_inv = tile("share_inv", [P, 1], F32)
-        nc.vector.reciprocal(share_inv[:], lm_divisor[:])
-
         def weights(name, lo, hi, tag=None):
             p = tile(name, [P, hi - lo], F32, tag=tag)
             p_sum = tile(name + "_sum", [P, 1], F32)
@@ -196,7 +178,7 @@ def tile_attend_knnlm_kernel(tc, query, keys_words, keys_scales, kn, hid, voc, l
         def places(lo, hi):
             return wf[:].indirect(place_list[:, lo // LANES : hi // LANES])
 
-        p_head, p_head_sum = weights("p_head", 0, I - TAIL, tag="voc1_raw")
+        p_head, p_head_sum = weights("p_head", 0, I - TAIL)
         act_copy(places(0, I - TAIL), p_head[:])
 
         low_first = lowest(tile("low_first", [P, 1], F32)[:], 0, b_first, None)
@@ -206,11 +188,17 @@ def tile_attend_knnlm_kernel(tc, query, keys_words, keys_scales, kn, hid, voc, l
         low_early = lowest(tile("low_early", [P, 1], F32)[:], FIRST, b_middle, low_first)
         b_last = multiply("last", last_bf)
         p_tail, p_tail_sum = weights("p_tail", I - TAIL, I, tag="voc3_raw")
-        p_total = tile("p_total", [P, 1], F32)
-        nc.scalar.activation(out=p_total[:], in_=p_head_sum[:], func=ACT.Identity, bias=p_tail_sum[:])
+        divisors = tile("divisors", [P, 2], F32)
+        knn_share = tile("knn_share", [P, 1], F32)
+        lm_share = tile("lm_share", [P, 1], F32)
+        nc.scalar.activation(out=lm_share[:], in_=lam_sb[:], func=ACT.Copy, scale=-512.0, bias=512.0)
+        nc.scalar.activation(out=knn_share[:], in_=lam_sb[:], func=ACT.Copy, scale=512.0)
+        nc.scalar.activation(out=divisors[:, 1:2], in_=lm_share[:], func=ACT.Copy, bias=SMALLEST_SHARE)
+        nc.scalar.activation(out=divisors[:, 0:1], in_=p_head_sum[:], func=ACT.Identity, bias=p_tail_sum[:])
         nc.vector.tensor_copy(places(I - TAIL, I), p_tail[:])
-        p_inv = tile("p_inv", [P, 1], F32)
-        nc.vector.reciprocal(p_inv[:], p_total[:])
+        inverses = tile("inverses", [P, 2], F32)
+        nc.vector.reciprocal(inverses[:], divisors[:])
+        p_inv, share_inv = inverses[:, 0:1], inverses[:, 1:2]
 
         r_sb = tile("r_sb", [P, V], F32)
         sum_early = tile("sum_early", [P, 1], F32)
@@ -219,10 +207,10 @@ def tile_attend_knnlm_kernel(tc, query, keys_words, keys_scales, kn, hid, voc, l
             out=r_sb[:, 0:EARLY], in_=neg_b[:, 0:EARLY], func=ACT.Exp, scale=-1.0, bias=low_early, accum_out=sum_early[:]
         )
         early_over_share = tile("early_over_share", [P, 1], F32)
-        nc.scalar.activation(out=early_over_share[:], in_=sum_early[:], func=ACT.Copy, scale=share_inv[:])
+        nc.scalar.activation(out=early_over_share[:], in_=sum_early[:], func=ACT.Copy, scale=share_inv)
         low_last = lowest(tile("low_last", [P, 1], F32)[:], EARLY, b_last, low_early)
         knn_part = tile("knn_part", [P, V], F32, tag="last_codes")
-        nc.vector.tensor_scalar(knn_part[:], wf[:], p_inv[:], knn_share[:], ALU.mult, ALU.mult)
+        nc.vector.tensor_scalar(knn_part[:], wf[:], p_inv, knn_share[:], ALU.mult, ALU.mult)
         shrink = tile("shrink", [P, 1], F32)
         nc.scalar.activation(out=shrink[:], in_=low_early, func=ACT.Exp, scale=-1.0, bias=low_last)
         nc.scalar.activation(
@@ -232,7 +220,7 @@ def tile_attend_knnlm_kernel(tc, query, keys_words, keys_scales, kn, hid, voc, l
         nc.scalar.activation(out=early_term[:], in_=early_over_share[:], func=ACT.Copy, scale=shrink[:])
         sum_over_share = tile("sum_over_share", [P, 1], F32)
         nc.scalar.activation(
-            out=sum_over_share[:], in_=sum_last[:], func=ACT.Identity, scale=share_inv[:], bias=early_term[:]
+            out=sum_over_share[:], in_=sum_last[:], func=ACT.Identity, scale=share_inv, bias=early_term[:]
         )
         factor_last = tile("factor_last", [P, 1], F32)
         nc.vector.reciprocal(factor_last[:], sum_over_share[:])

@@ -22,7 +22,6 @@ PACK = 4
 LANES = 16
 KN_ROW = P - 1
 CHUNKS = ((0, 256), (256, 512), (512, 768), (768, 1024))
-FIRST = 256
 EARLY = 768
 PIECE = 256
 TAIL = 128
@@ -150,11 +149,13 @@ def tile_attend_knnlm_kernel(tc, query, keys_words, keys_scales, kn, hid, voc, l
 
         neg_b = tile("neg_b", [P, V], F32)
 
-        def multiply(name, grouped):
+        b_first = ps.tile([P, PIECE], F32, name="b_first")
+        b_middle = ps.tile([P, 2 * PIECE], F32, name="b_middle")
+        b_last = ps.tile([P, PIECE], F32, name="b_last")
+
+        def multiply(name, grouped, logits):
             codes, scales = quantize(name, grouped)
-            b_ps = ps.tile([P, grouped.shape[1]], F32, name=name + "_ps")
-            product(b_ps[:], (hid_codes[:], hid_scales[:]), (codes[:], scales[:]))
-            return b_ps
+            product(logits, (hid_codes[:], hid_scales[:]), (codes[:], scales[:]))
 
         def lowest(low, lo, b_ps, start):
             nc.vector.tensor_scalar(
@@ -162,10 +163,8 @@ def tile_attend_knnlm_kernel(tc, query, keys_words, keys_scales, kn, hid, voc, l
             )
             return low
 
-        b_first = multiply("first", cast("voc0", voc_raw[0], nc.vector.tensor_copy))
-        middle_bf = tile("middle_bf", [P, EARLY - FIRST, PACK], BF16)
-        cut = voc_raw[1].shape[2]
-        interleave(act_copy, middle_bf[:, 0:cut, :], voc_raw[1][:])
+        multiply("voc0", cast("voc0", voc_raw[0], nc.vector.tensor_copy), b_first[:])
+        voc1_bf = cast("voc1", voc_raw[1], act_copy)
         neg_max = tile("neg_max", [P, 1], F32, tag="voc0_raw")
         nc.vector.tensor_reduce(out=neg_max[:], in_=s_ps[:], axis=AX.X, op=ALU.max, negate=True)
 
@@ -182,24 +181,24 @@ def tile_attend_knnlm_kernel(tc, query, keys_words, keys_scales, kn, hid, voc, l
         act_copy(places(0, I - TAIL), p_head[:])
 
         low_first = lowest(tile("low_first", [P, 1], F32)[:], 0, b_first, None)
-        interleave(nc.vector.tensor_copy, middle_bf[:, cut:, :], voc_raw[2][:])
-        b_middle = multiply("middle", middle_bf)
-        last_bf = cast("voc3", voc_raw[3], nc.vector.tensor_copy)
-        low_early = lowest(tile("low_early", [P, 1], F32)[:], FIRST, b_middle, low_first)
-        b_last = multiply("last", last_bf)
-        p_tail, p_tail_sum = weights("p_tail", I - TAIL, I, tag="voc3_raw")
-        divisors = tile("divisors", [P, 2], F32)
+        voc2_bf = cast("voc2", voc_raw[2], nc.vector.tensor_copy)
+        multiply("voc1", voc1_bf, b_middle[:, 0:PIECE])
+        multiply("voc2", voc2_bf, b_middle[:, PIECE:])
+        multiply("voc3", cast("voc3", voc_raw[3], nc.vector.tensor_copy), b_last[:])
+        low_early = lowest(tile("low_early", [P, 1], F32, tag="voc3_raw")[:], PIECE, b_middle, low_first)
+        p_tail, p_tail_sum = weights("p_tail", I - TAIL, I, tag="voc3_codes")
+        lm_divisor = tile("lm_divisor", [P, 1], F32)
+        p_total = tile("p_total", [P, 1], F32)
         knn_share = tile("knn_share", [P, 1], F32)
         lm_share = tile("lm_share", [P, 1], F32)
         nc.scalar.activation(out=lm_share[:], in_=lam_sb[:], func=ACT.Copy, scale=-512.0, bias=512.0)
         nc.scalar.activation(out=knn_share[:], in_=lam_sb[:], func=ACT.Copy, scale=512.0)
-        nc.scalar.activation(out=divisors[:, 1:2], in_=lm_share[:], func=ACT.Copy, bias=SMALLEST_SHARE)
-        nc.scalar.activation(out=divisors[:, 0:1], in_=p_head_sum[:], func=ACT.Identity, bias=p_tail_sum[:])
-        nc.vector.tensor_copy(places(I - TAIL, I), p_tail[:])
-        inverses = tile("inverses", [P, 2], F32)
-        nc.vector.reciprocal(inverses[:], divisors[:])
-        p_inv, share_inv = inverses[:, 0:1], inverses[:, 1:2]
+        nc.scalar.activation(out=lm_divisor[:], in_=lm_share[:], func=ACT.Copy, bias=SMALLEST_SHARE)
+        nc.scalar.activation(out=p_total[:], in_=p_head_sum[:], func=ACT.Identity, bias=p_tail_sum[:])
 
+        low_last = lowest(tile("low_last", [P, 1], F32)[:], EARLY, b_last, low_early)
+        share_inv = tile("share_inv", [P, 1], F32, tag="low_first")[:]
+        nc.vector.reciprocal(share_inv, lm_divisor[:])
         r_sb = tile("r_sb", [P, V], F32)
         sum_early = tile("sum_early", [P, 1], F32)
         sum_last = tile("sum_last", [P, 1], F32)
@@ -208,9 +207,15 @@ def tile_attend_knnlm_kernel(tc, query, keys_words, keys_scales, kn, hid, voc, l
         )
         early_over_share = tile("early_over_share", [P, 1], F32)
         nc.scalar.activation(out=early_over_share[:], in_=sum_early[:], func=ACT.Copy, scale=share_inv)
-        low_last = lowest(tile("low_last", [P, 1], F32)[:], EARLY, b_last, low_early)
-        knn_part = tile("knn_part", [P, V], F32, tag="last_codes")
-        nc.vector.tensor_scalar(knn_part[:], wf[:], p_inv, knn_share[:], ALU.mult, ALU.mult)
+        nc.vector.tensor_copy(places(I - TAIL, I), p_tail[:])
+        p_inv = tile("p_inv", [P, 1], F32)[:]
+        nc.vector.reciprocal(p_inv, p_total[:])
+        def normalise(name, lo, hi, tag=None):
+            part = tile(name, [P, hi - lo], F32, tag=tag)
+            nc.vector.tensor_scalar(part[:], wf[:, lo:hi], p_inv, knn_share[:], ALU.mult, ALU.mult)
+            return part
+
+        knn_high = normalise("knn_high", V // 2, V)
         shrink = tile("shrink", [P, 1], F32)
         nc.scalar.activation(out=shrink[:], in_=low_early, func=ACT.Exp, scale=-1.0, bias=low_last)
         nc.scalar.activation(
@@ -224,14 +229,16 @@ def tile_attend_knnlm_kernel(tc, query, keys_words, keys_scales, kn, hid, voc, l
         )
         factor_last = tile("factor_last", [P, 1], F32)
         nc.vector.reciprocal(factor_last[:], sum_over_share[:])
+        knn_low = normalise("knn_low", 0, V // 2, tag="early_term")
         factor_early = tile("factor_early", [P, 1], F32)
         nc.scalar.activation(out=factor_early[:], in_=factor_last[:], func=ACT.Copy, scale=shrink[:])
 
-        for c in (3, 0, 1, 2):
+        for c in (3, 2, 0, 1):
             lo, hi = c * PIECE, (c + 1) * PIECE
             factor = factor_last if lo >= EARLY else factor_early
+            knn = knn_high[:, lo - V // 2 : hi - V // 2] if lo >= V // 2 else knn_low[:, lo:hi]
             mixed = tile("mixed%d" % c, [P, PIECE], F32)
             nc.vector.scalar_tensor_tensor(
-                out=mixed[:], in0=r_sb[:, lo:hi], scalar=factor[:], in1=knn_part[:, lo:hi], op0=ALU.mult, op1=ALU.add
+                out=mixed[:], in0=r_sb[:, lo:hi], scalar=factor[:], in1=knn, op0=ALU.mult, op1=ALU.add
             )
             nc.sync.dma_start(out=out[:, lo:hi], in_=mixed[:])

@@ -184,21 +184,33 @@ def tile_attend_knnlm_kernel(tc, query, keys_words, keys_scales, kn, hid, voc, l
         voc2_bf = cast("voc2", voc_raw[2], nc.vector.tensor_copy)
         multiply("voc1", voc1_bf, b_middle[:, 0:PIECE])
         multiply("voc2", voc2_bf, b_middle[:, PIECE:])
-        multiply("voc3", cast("voc3", voc_raw[3], nc.vector.tensor_copy), b_last[:])
+        last_bf = tile("voc3_bf", [P, PIECE, PACK], BF16)
+        last_codes = tile("voc3_codes", [P, PIECE], U32)
+        last_scales = tile("voc3_scales", [P, PIECE], U8)
+        halves = (slice(0, PIECE // 2), slice(PIECE // 2, PIECE))
+        for cols in halves:
+            interleave(nc.vector.tensor_copy, last_bf[:, cols, :], voc_raw[3][:, :, cols])
+        for cols in halves:
+            nc.vector.quantize_mx(
+                out=last_codes[:, cols].bitcast(FP8X4),
+                scales=last_scales[:, cols],
+                in_=last_bf[:, cols, :].rearrange("p w t -> p (w t)"),
+            )
+        product(b_last[:], (hid_codes[:], hid_scales[:]), (last_codes[:], last_scales[:]))
         low_early = lowest(tile("low_early", [P, 1], F32, tag="voc3_raw")[:], PIECE, b_middle, low_first)
         p_tail, p_tail_sum = weights("p_tail", I - TAIL, I, tag="voc3_codes")
         lm_divisor = tile("lm_divisor", [P, 1], F32)
         p_total = tile("p_total", [P, 1], F32)
         knn_share = tile("knn_share", [P, 1], F32)
         lm_share = tile("lm_share", [P, 1], F32)
-        nc.scalar.activation(out=lm_share[:], in_=lam_sb[:], func=ACT.Copy, scale=-512.0, bias=512.0)
-        nc.scalar.activation(out=knn_share[:], in_=lam_sb[:], func=ACT.Copy, scale=512.0)
-        nc.scalar.activation(out=lm_divisor[:], in_=lm_share[:], func=ACT.Copy, bias=SMALLEST_SHARE)
-        nc.scalar.activation(out=p_total[:], in_=p_head_sum[:], func=ACT.Identity, bias=p_tail_sum[:])
+        nc.vector.tensor_scalar(lm_share[:], lam_sb[:], -512.0, 512.0, ALU.mult, ALU.add)
+        nc.vector.tensor_scalar(knn_share[:], lam_sb[:], 512.0, None, ALU.mult)
+        nc.vector.tensor_scalar(lm_divisor[:], lm_share[:], SMALLEST_SHARE, None, ALU.add)
 
         low_last = lowest(tile("low_last", [P, 1], F32)[:], EARLY, b_last, low_early)
         share_inv = tile("share_inv", [P, 1], F32, tag="low_first")[:]
         nc.vector.reciprocal(share_inv, lm_divisor[:])
+        nc.vector.tensor_scalar(p_total[:], p_head_sum[:], p_tail_sum[:], None, ALU.add)
         r_sb = tile("r_sb", [P, V], F32)
         sum_early = tile("sum_early", [P, 1], F32)
         sum_last = tile("sum_last", [P, 1], F32)
@@ -210,6 +222,7 @@ def tile_attend_knnlm_kernel(tc, query, keys_words, keys_scales, kn, hid, voc, l
         nc.vector.tensor_copy(places(I - TAIL, I), p_tail[:])
         p_inv = tile("p_inv", [P, 1], F32)[:]
         nc.vector.reciprocal(p_inv, p_total[:])
+
         def normalise(name, lo, hi, tag=None):
             part = tile(name, [P, hi - lo], F32, tag=tag)
             nc.vector.tensor_scalar(part[:], wf[:, lo:hi], p_inv, knn_share[:], ALU.mult, ALU.mult)

from contextlib import ExitStack

import concourse.mybir as mybir
from concourse.masks import make_identity

D, K, T, I, V, Q = 512, 512, 2048, 512, 1024, 128
FLOPS = 2 * D * Q * I + 2 * K * Q * V

F32 = mybir.dt.float32
BF16 = mybir.dt.bfloat16
I32 = mybir.dt.int32
U32 = mybir.dt.uint32
U16 = mybir.dt.uint16
U8 = mybir.dt.uint8
FP8X4 = mybir.dt.float8_e4m3fn_x4
ALU = mybir.AluOpType
ACT = mybir.ActivationFunctionType
AX = mybir.AxisListType

P = 128
PACK = 4
LANES = 16
KN_ROW = P - 1
CHUNKS = ((0, 256), (256, 512), (512, 768), (768, 1024))
EARLY = 768
PIECE = 256
TAIL = 128
HALF = I // 2
SMALLEST_SHARE = 2.0**-64


def tile_attend_knnlm_kernel(tc, query, keys_words, keys_scales, kn, hid, voc, lam, offs, offs2, out):
    nc = tc.nc
    with ExitStack() as ctx:
        sb = ctx.enter_context(tc.tile_pool(name="sb", bufs=1))
        ps = ctx.enter_context(tc.psum_pool(name="ps", bufs=1))

        def tile(name, shape, dtype, tag=None):
            return sb.tile(shape, dtype, name=name, tag=tag or name, align_bytes=64)

        def load_rows(name, rows):
            raw = tile(name + "_raw", [P, PACK, rows.shape[1]], F32)
            nc.sync.dma_start(out=raw[:], in_=rows.rearrange("(p j) w -> p j w", j=PACK))
            return raw

        def act_copy(out, in_):
            nc.scalar.activation(out=out, in_=in_, func=ACT.Copy)

        def interleave(copy, grouped, raw):
            copy(
                out=grouped.rearrange("p (c i) t -> p c t i", i=4),
                in_=raw.rearrange("p t (c i) -> p c t i", i=4),
            )

        def cast(name, raw, copy):
            grouped = tile(name + "_bf", [P, raw.shape[2], PACK], BF16)
            interleave(copy, grouped[:], raw[:])
            return grouped

        def quantize(name, grouped):
            width = grouped.shape[1]
            codes = tile(name + "_codes", [P, width], U32)
            scales = tile(name + "_scales", [P, width], U8)
            nc.vector.quantize_mx(
                out=codes[:].bitcast(FP8X4), scales=scales[:], in_=grouped[:].rearrange("p w t -> p (w t)")
            )
            return codes, scales

        def product(out_ps, stationary, moving):
            nc.tensor.matmul_mx(
                out=out_ps,
                lhsT=stationary[0].bitcast(FP8X4),
                lhsT_scale=stationary[1],
                rhs=moving[0].bitcast(FP8X4),
                rhs_scale=moving[1],
                start=True,
                stop=True,
            )

        scale_pool = tile("scale_pool", [P, T], U8)
        kn_pool = tile("kn_pool", [P, T], F32)
        word_pool = tile("word_pool", [P, T], I32)
        ident = tile("ident", [P, P], F32)
        key_list = tile("key_list", [P, I // LANES], U16)
        place_list = tile("place_list", [P, I // LANES], U16)
        wf = tile("wf", [P, V], F32)

        nc.vector.memset(scale_pool[:].bitcast(I32), 0)
        nc.vector.memset(ident[:], 0.0)
        make_identity(nc, ident[:], nomemset=True)
        nc.vector.memset(kn_pool[0:KN_ROW, :].bitcast(I32), 0)
        nc.vector.memset(wf[:].bitcast(I32), 0)

        query_raw = load_rows("query", query)
        nc.sync.dma_start(key_list[:], offs)
        nc.sync.dma_start(out=kn_pool[KN_ROW:P, :], in_=kn[0:1, :])
        for row in range(4):
            nc.sync.dma_start(
                out=scale_pool[row:P:32, :].bitcast(I32), in_=keys_scales[0, row:16:4, :].bitcast(I32)
            )
        nc.sync.dma_start(out=word_pool[:], in_=keys_words[0].rearrange("p n t -> p (n t)").bitcast(I32))
        hid_raw = load_rows("hid", hid)
        voc_raw = []
        lam_sb = tile("lam_sb", [P, 1], F32)
        for c, (lo, hi) in enumerate(CHUNKS):
            voc_raw.append(load_rows("voc%d" % c, voc[:, lo:hi]))
            if c == 2:
                nc.sync.dma_start(place_list[:], offs2)
        nc.sync.dma_start(out=lam_sb[:], in_=lam)

        query_bf = cast("query", query_raw, act_copy)
        kn_listed = tile("kn_listed", [P, I], F32, tag="query_raw")
        neg_kn = tile("neg_kn", [P, I // P], F32)
        blocks = HALF // P
        for h in range(2):
            lo = h * HALF
            act_copy(kn_listed[:, lo : lo + HALF], kn_pool[:].indirect(key_list[:, lo // LANES : (lo + HALF) // LANES]))
        for h in range(2):
            kn_turned = ps.tile([P, blocks, P], F32, name="kn_turned%d" % h, tag="a_bank%d" % (h * blocks))
            for u in range(blocks):
                lo = (h * blocks + u) * P
                nc.tensor.transpose(kn_turned[:, u, :], kn_listed[:, lo : lo + P], ident[:])
            nc.scalar.activation(
                out=neg_kn[:, h * blocks : (h + 1) * blocks], in_=kn_turned[:, :, KN_ROW], func=ACT.Copy, scale=-1.0
            )

        key_scales = tile("key_scales", [P, I], U8)
        nc.vector.tensor_copy(key_scales[:], scale_pool[:].indirect(key_list[:]))
        query_codes, query_scales = quantize("query", query_bf)

        hid_bf = cast("hid", hid_raw, act_copy)
        s_turned = tile("s_turned", [P, I // P, Q], F32, tag="hid_raw")
        s_ps = ps.tile([P, I], F32, name="s_ps")
        for j in range(I // P):
            lo = j * P
            key_words = tile("key_words%d" % j, [P, P], I32)
            nc.vector.tensor_copy(
                key_words[:].bitcast(U32),
                word_pool[:].bitcast(U32).indirect(key_list[:, lo // LANES : (lo + P) // LANES]),
            )
            a_ps = ps.tile([P, Q], F32, name="a_ps%d" % j, tag="a_bank%d" % j)
            product(a_ps[:], (key_words[:], key_scales[:, lo : lo + P]), (query_codes[:], query_scales[:]))
            nc.scalar.activation(
                out=s_turned[:, j, :], in_=a_ps[:], func=ACT.Identity, scale=2.0, bias=neg_kn[:, j : j + 1]
            )
            nc.tensor.transpose(s_ps[:, lo : lo + P], s_turned[:, j, :], ident[:])

        hid_codes, hid_scales = quantize("hid", hid_bf)

        neg_b = tile("neg_b", [P, V], F32)

        b_first = ps.tile([P, PIECE], F32, name="b_first")
        b_middle = ps.tile([P, 2 * PIECE], F32, name="b_middle")
        b_last = ps.tile([P, PIECE], F32, name="b_last")

        def multiply(name, grouped, logits):
            codes, scales = quantize(name, grouped)
            product(logits, (hid_codes[:], hid_scales[:]), (codes[:], scales[:]))

        def lowest(low, lo, b_ps, start):
            nc.vector.tensor_scalar(
                neg_b[:, lo : lo + b_ps.shape[1]], b_ps[:], -1.0, start, ALU.mult, ALU.min, accum_out=low
            )
            return low

        multiply("voc0", cast("voc0", voc_raw[0], nc.vector.tensor_copy), b_first[:])
        voc1_bf = cast("voc1", voc_raw[1], act_copy)
        neg_max = tile("neg_max", [P, 1], F32, tag="voc0_raw")
        nc.vector.tensor_reduce(out=neg_max[:], in_=s_ps[:], axis=AX.X, op=ALU.max, negate=True)

        def weights(name, lo, hi, tag=None):
            p = tile(name, [P, hi - lo], F32, tag=tag)
            p_sum = tile(name + "_sum", [P, 1], F32)
            nc.scalar.activation(out=p[:], in_=s_ps[:, lo:hi], func=ACT.Exp, bias=neg_max[:], accum_out=p_sum[:])
            return p, p_sum

        def places(lo, hi):
            return wf[:].indirect(place_list[:, lo // LANES : hi // LANES])

        p_head, p_head_sum = weights("p_head", 0, I - TAIL)
        act_copy(places(0, I - TAIL), p_head[:])

        low_first = lowest(tile("low_first", [P, 1], F32)[:], 0, b_first, None)
        voc2_bf = cast("voc2", voc_raw[2], nc.vector.tensor_copy)
        multiply("voc1", voc1_bf, b_middle[:, 0:PIECE])
        multiply("voc2", voc2_bf, b_middle[:, PIECE:])
        last_bf = tile("voc3_bf", [P, PIECE, PACK], BF16)
        last_codes = tile("voc3_codes", [P, PIECE], U32)
        last_scales = tile("voc3_scales", [P, PIECE], U8)
        halves = (slice(0, PIECE // 2), slice(PIECE // 2, PIECE))
        for cols in halves:
            interleave(nc.vector.tensor_copy, last_bf[:, cols, :], voc_raw[3][:, :, cols])
        for cols in halves:
            nc.vector.quantize_mx(
                out=last_codes[:, cols].bitcast(FP8X4),
                scales=last_scales[:, cols],
                in_=last_bf[:, cols, :].rearrange("p w t -> p (w t)"),
            )
        product(b_last[:], (hid_codes[:], hid_scales[:]), (last_codes[:], last_scales[:]))
        low_early = lowest(tile("low_early", [P, 1], F32, tag="voc3_raw")[:], PIECE, b_middle, low_first)
        p_tail, p_tail_sum = weights("p_tail", I - TAIL, I, tag="voc3_codes")
        lm_divisor = tile("lm_divisor", [P, 1], F32)
        p_total = tile("p_total", [P, 1], F32)
        knn_share = tile("knn_share", [P, 1], F32)
        lm_share = tile("lm_share", [P, 1], F32)
        nc.vector.tensor_scalar(lm_share[:], lam_sb[:], -512.0, 512.0, ALU.mult, ALU.add)
        nc.vector.tensor_scalar(knn_share[:], lam_sb[:], 512.0, None, ALU.mult)
        nc.vector.tensor_scalar(lm_divisor[:], lm_share[:], SMALLEST_SHARE, None, ALU.add)

        low_last = lowest(tile("low_last", [P, 1], F32)[:], EARLY, b_last, low_early)
        share_inv = tile("share_inv", [P, 1], F32, tag="low_first")[:]
        nc.vector.reciprocal(share_inv, lm_divisor[:])
        nc.vector.tensor_scalar(p_total[:], p_head_sum[:], p_tail_sum[:], None, ALU.add)
        r_sb = tile("r_sb", [P, V], F32)
        sum_early = tile("sum_early", [P, 1], F32)
        sum_last = tile("sum_last", [P, 1], F32)
        nc.scalar.activation(
            out=r_sb[:, 0:EARLY], in_=neg_b[:, 0:EARLY], func=ACT.Exp, scale=-1.0, bias=low_early, accum_out=sum_early[:]
        )
        early_over_share = tile("early_over_share", [P, 1], F32)
        nc.scalar.activation(out=early_over_share[:], in_=sum_early[:], func=ACT.Copy, scale=share_inv)
        nc.vector.tensor_copy(places(I - TAIL, I), p_tail[:])
        p_inv = tile("p_inv", [P, 1], F32)[:]
        nc.vector.reciprocal(p_inv, p_total[:])

        def normalise(name, lo, hi, tag=None):
            part = tile(name, [P, hi - lo], F32, tag=tag)
            nc.vector.tensor_scalar(part[:], wf[:, lo:hi], p_inv, knn_share[:], ALU.mult, ALU.mult)
            return part

        knn_high = normalise("knn_high", V // 2, V)
        shrink = tile("shrink", [P, 1], F32)
        nc.scalar.activation(out=shrink[:], in_=low_early, func=ACT.Exp, scale=-1.0, bias=low_last)
        nc.scalar.activation(
            out=r_sb[:, EARLY:V], in_=neg_b[:, EARLY:V], func=ACT.Exp, scale=-1.0, bias=low_last, accum_out=sum_last[:]
        )
        early_term = tile("early_term", [P, 1], F32)
        nc.scalar.activation(out=early_term[:], in_=early_over_share[:], func=ACT.Copy, scale=shrink[:])
        sum_over_share = tile("sum_over_share", [P, 1], F32)
        nc.scalar.activation(
            out=sum_over_share[:], in_=sum_last[:], func=ACT.Identity, scale=share_inv, bias=early_term[:]
        )
        factor_last = tile("factor_last", [P, 1], F32)
        nc.vector.reciprocal(factor_last[:], sum_over_share[:])
        knn_low = normalise("knn_low", 0, V // 2, tag="early_term")
        factor_early = tile("factor_early", [P, 1], F32)
        nc.scalar.activation(out=factor_early[:], in_=factor_last[:], func=ACT.Copy, scale=shrink[:])

        for c in (3, 2, 0, 1):
            lo, hi = c * PIECE, (c + 1) * PIECE
            factor = factor_last if lo >= EARLY else factor_early
            knn = knn_high[:, lo - V // 2 : hi - V // 2] if lo >= V // 2 else knn_low[:, lo:hi]
            mixed = tile("mixed%d" % c, [P, PIECE], F32)
            nc.vector.scalar_tensor_tensor(
                out=mixed[:], in0=r_sb[:, lo:hi], scalar=factor[:], in1=knn, op0=ALU.mult, op1=ALU.add
            )
            nc.sync.dma_start(out=out[:, lo:hi], in_=mixed[:])
